import numpy as np, ml_dtypes
CORES = [9,25,41,57]
N = 4
import mx_ref
BF = ml_dtypes.bfloat16
def gcols(t, e):
    v = np.concatenate([t.reshape(8, 16, -1, 4), np.zeros((8, 16, 1, 4), BF)], axis=2)
    return np.ascontiguousarray(np.stack([v[g][:, e[g]] for g in range(8)])).reshape(128, -1)
def tile(rs):
    return np.stack(rs, axis=2).reshape(128, -1).astype(BF)
def pick(q, e):
    c = np.concatenate([q[0].reshape(128, -1, 4), np.zeros((128, 1, 4), np.uint8)], axis=1); s = np.concatenate([q[1], np.ones((16, 1), np.uint8)], axis=1)
    return (np.ascontiguousarray(c[:, e].reshape(128, -1)), np.ascontiguousarray(s[:, e]))
def join(*qs):
    return (np.concatenate([q[0] for q in qs], axis=1), np.concatenate([q[1] for q in qs], axis=1))
def put(q, e, v):
    c, s = q[0].reshape(128, -1, 4).copy(), q[1].copy(); c[:, e] = v[0].reshape(128, -1, 4); s[:, e] = v[1]
    return (c.reshape(128, -1), s)
def pk(c, s):
    return (np.ascontiguousarray(c), mx_ref.live(s))
def emit(q):
    return q[0], q[1]
def packed(v, rng):
    q = [mx_ref.quantize(np.ascontiguousarray(v[r])) for r in range(N)]
    return np.stack([a for a, b in q]), np.stack([mx_ref.plane(b, rng) for a, b in q])
def values_of_codes():
    e, c = np.zeros((128, 128, 4), np.float32), np.zeros((128, 2, 4), np.uint8)
    e[np.arange(128), np.arange(128), 0] = 1
    c[:127, :, 0] = np.arange(256).reshape(2, 128).T[:127]
    return mx_ref.matmul(mx_ref.quantize(e.reshape(128, 512).astype(BF)), (c.reshape(128, 8), np.full((16, 2), 127, np.uint8))).T.reshape(-1).astype(np.float64)
CODE_VALUE, SCALE_VALUE = values_of_codes(), 2.0 ** (np.arange(256) - 127.0)
def decode(q):
    return (CODE_VALUE[q[0]].reshape(16, 8, -1, 4) * SCALE_VALUE[q[1]][:, None, :, None] + 0.0).reshape(128, -1).astype(np.float32)
def f(rng, *shape):
    return mx_ref.flush((rng.standard_normal(shape, dtype=np.float32) * np.exp2(rng.integers(-2, 3, shape[:-1] + (1,)))).astype(BF))
def wide(rng, *shape, cols=0):
    v = rng.standard_normal(shape, dtype=np.float32) * np.exp2(rng.integers(-12, 13, shape)).astype(np.float32)
    if cols: v *= np.repeat(np.exp2(rng.integers(-cols, cols + 1, shape[:-2] + (1, shape[-1] // 4))) * (rng.random(shape[:-2] + (1, shape[-1] // 4)) > 0.0625), 4, axis=-1).astype(np.float32)
    return mx_ref.flush(v.astype(BF))
C, K, M, S, H = 320, 64, 5, 14, 160
PARTNER = [1, 2, 3]
COL = np.stack([M * ((np.arange(K) + 8 * g) % K)[:, None] + np.arange(M) for g in range(8)])
CLOCK = np.stack([(np.arange(C) // M - 8 * g) % K for g in range(8)])
def big(v):
    v = v.astype(np.float32)
    v[np.abs(v) < np.float32(2.0 ** -20)] = 0
    return v.astype(BF)
def numbers_of(rng):
    return {"x": big(f(rng, N, 128, 4 * C)), "u": np.array(f(rng, N, 128, 512)), "v": np.array(f(rng, N, 128, 512))}
def weights(rng, w):
    c, s = packed(np.ascontiguousarray(w.reshape(N, 128, 4, 512).transpose(0, 1, 3, 2)).reshape(N, 128, 2048).astype(BF), rng)
    return {"wc": c, "ws": s}
def layers(rng, still=()):
    w = np.zeros((N, 512, 512), np.float32)
    for r in range(N): w[r, rng.integers(0, 512, (24, 512)), np.arange(512)] = rng.choice([-1.0, 1.0], (24, 512)) * (16 + 20 * rng.random((24, 512)))
    w = w.reshape(N, 8, 16, 4, 512)
    for i in still:
        w[:, :, i] = 0
        w[..., i::16] = 0
    return weights(rng, w.reshape(N, 512, 512))
def setup_inputs(rng):
    return {**numbers_of(rng), **layers(rng)}
def setup_inputs_ties(rng):
    d = numbers_of(rng)
    o = rng.permutation(N)
    x = d["x"].reshape(N, 8, 16, C, 4)
    s = rng.integers(-1, 2, (N, 8, C, 4)).astype(np.float32)
    s[..., 3] -= 1
    s[o[0]] = 0
    s[o[1], :, :, :3] = 1
    for g in range(8): s[o[2], g, :, :3] = [2.0 * (g >> 2 & 1) - 1, 2.0 * (g >> 1 & 1) - 1, 2.0 * (g & 1) - 1]
    x[:, :, 0] = s.astype(BF)
    e = (N, 8, 8, C, 4)
    x[:, :, 8:] = (rng.choice([-1.0, 1.0], e) * (1 + (2 * rng.integers(0, 64, e) + 1) * 2.0 ** -7) * np.exp2(-rng.integers(8, 15, e).astype(np.float64))).astype(np.float32).astype(BF)
    x[:, :, 8, :, 0] = 1.96875
    u = d["u"].reshape(N, 128, 128, 4)
    for b in range(4): u[:, :, b::16] = 0
    for h in range(0, 128, 16):
        for b in range(4): u[:, h, h + b, b] = 1
    return {"x": x.reshape(N, 128, 4 * C), "u": u.reshape(N, 128, 512), "v": d["v"], **layers(rng, [0])}
def setup_inputs_near(rng):
    d = numbers_of(rng)
    o = rng.permutation(N) % 2
    x = d["x"].astype(np.float32).reshape(N, 8, 16, C, 4)
    x[:, :, 0] = 0
    x[:, :, 8:] = 0
    u = d["u"].reshape(N, 128, 128, 4)
    for b in range(4): u[:, :, b::16] = 0
    for r in range(N):
        a = rng.integers(-1, 2, (8, C, 3)).astype(np.float32)
        k = rng.choice([-1.0, 1.0], (8, 1))
        if o[r] == 0:
            s = rng.integers(0, 16, (8, C))
            x[r, :, 0, :, :3] = a
            x[r, :, 0, :, 3] = k
            x[r, :, 8] = ((s[:, :, None] >> np.arange(4)) & 1) * np.exp2(np.arange(4) - 23.0)
            x[r, :, 11, :, 0] = 2.0 ** -10
        else:
            x[r, :, 8, :, :3] = a * np.float32(1.125 * 2.0 ** -24)
            x[r, :, 9, :, :3] = a * np.float32(2.0 ** -24)
            e = rng.integers(0, 4, (8, C))
            x[r, :, 10, :, 3] = k * np.array([1.125, 1.375, 0, 0])[e] * 2.0 ** -24 + 0.0
            x[r, :, 12, :, 3] = k * np.array([0, 0, 1.0, 1.25])[e] * 2.0 ** -24 + 0.0
            for g in rng.permutation(8)[:4]: x[r, g, 10, rng.integers(C), 3] = 2.0 ** 29 * rng.choice([-1.0, 1.0])
        for h in range(0, 128, 16):
            if o[r] == 0:
                for b in range(4): u[r, h, h + b, b] = 1
                u[r, h + 8, h + 3] = 1
                u[r, h + 11, h + 3, 0] = 1
            else:
                for b in range(3):
                    u[r, h + 8, h + b, b] = 1.125 * 2.0 ** -30
                    u[r, h + 9, h + b, b] = -1.25 * 2.0 ** -30
                u[r, h + 10, h + 3, 3] = 1.125 * 2.0 ** -30
                u[r, h + 12, h + 3, 3] = 1.25 * 2.0 ** -30
    return {"x": x.reshape(N, 128, 4 * C).astype(BF), "u": u.reshape(N, 128, 512), "v": d["v"], **layers(rng, [0, 8, 9, 10, 11, 12, 13, 14, 15])}
def setup_inputs_twice(rng):
    d = numbers_of(rng)
    e = (N, 8, 16, C, 4)
    x = rng.choice([-1.0, 1.0], e) * (1 + (2 * rng.integers(0, 64, e) + 1) * 2.0 ** -7) * np.exp2(-rng.integers(13, 15, e).astype(np.float64))
    x[:, :, 0] = 0
    x[:, :, 0, :, 0] = 1.96875 * rng.choice([-1.0, 1.0], (N, 8, C))
    x[:, :, 8] = 0
    x[:, :4, 8, :, 0] = rng.choice([3.25, 0.6875], (N, 4, C))
    x[:, 4:, 8:] = 0
    u = d["u"].reshape(N, 128, 128, 4)
    u[:, :, 3::16] = 0
    for h in range(0, 128, 16): u[:, h + 1:h + 8, h + 3, 0] = 1
    w = np.zeros((N, 512, 512), np.float32)
    i = np.arange(9, 16)
    for g in range(4, 8):
        for b in range(4): w[:, 4 * (16 * (g - 4) + i) + b, 128 * b + 16 * g + i] = 1024.0
    return {"x": x.astype(np.float32).reshape(N, 128, 4 * C).astype(BF), "u": u.reshape(N, 128, 512), "v": d["v"], **weights(rng, w)}
def setup_inputs_ends(rng):
    d = numbers_of(rng)
    e = rng.permutation(N)
    o = e % 4
    x = np.zeros((N, 8, 16, C, 4), np.float32)
    u = d["u"].reshape(N, 128, 128, 4)
    v = rng.choice([-1.0, 1.0], (N, 128, 512))
    w = np.zeros((N, 512, 512), np.float32)
    i = np.arange(128)
    for r in range(N):
        if o[r] == 0: x[r] = -2.0 ** 30 * (1 - 0.125 * rng.integers(0, 2, (8, 1, C, 1)))
        elif o[r] == 1: x[r] = 2.0 ** 30 * rng.choice([-1.0, 1.0], (1, 1, C, 1))
        elif o[r] == 2: x[r] = 2.0 ** -24
        else: x[r] = 2.0 ** 30 * rng.choice([-1.0, 1.0], (8, 16, C, 4))
        if e[r] == 0: x[r][:, :, np.isin(np.arange(C) // M % 8, rng.permutation(8)[:4])] = -2.0 ** 30
        if o[r] == 2:
            for b in range(4): u[r, :, b::16] = 2.0 ** -30
        else:
            for b in range(3): u[r, :, b::16] = (2.0 ** 30 * rng.choice([-1.0, 1.0], (128, 8, 4))).astype(np.float32).astype(BF)
            u[r, :, 3::16] = 2.0 ** 30 if e[r] == 0 or o[r] == 1 else 0.875 * 2.0 ** 30
            for h in range(0, 128, 16): u[r, h:h + 16, h + 3] = 2.0 ** 30
        v[r] *= 2.0 ** 30 if o[r] % 2 == 0 else 2.0 ** -30
        for b in range(4): w[r, 4 * i + b, 128 * b + i] = -1024.0 if o[r] == 1 else 1024.0
    return {"x": x.reshape(N, 128, 4 * C).astype(BF), "u": u.reshape(N, 128, 512), "v": v.astype(np.float32).astype(BF), **weights(rng, w)}
def setup_inputs_spread(rng):
    d = setup_inputs(rng)
    d["x"] = big(wide(rng, N, 128, 4 * C, cols=6))
    return d
def check_inputs(d):
    b = []
    for k, low in (("x", 2.0 ** -24), ("u", 2.0 ** -30), ("v", 2.0 ** -30)):
        a = np.abs(d[k].astype(np.float32))
        if not (np.isfinite(a).all() and ((a == 0) | (a >= low) & (a <= 2.0 ** 30)).all()): b.append("a value of " + k)
    none, least, most = [emit(mx_ref.quantize(np.full((128, 16), k, np.float32).astype(BF)))[1][0, 0] for k in (0.0, 2.0 ** -30, 2.0 ** 30)]
    for r in range(N):
        if ((d["wc"][r] == 0x7F) | (d["wc"][r] == 0xFF)).any(): b.append("wc: a code that is no number")
        s = mx_ref.live(d["ws"][r])
        if ((s != none) & ((s < least) | (s > most))).any(): b.append("ws: a scale out of range")
        with np.errstate(all="ignore"):
            a = np.sum(np.abs(decode(pk(d["wc"][r], d["ws"][r]))).astype(np.float64).reshape(128, 512, 4), axis=(0, 2))
            if not (a <= 1024).all(): b.append("sizes in a column of W")
    return b
def walk(s):
    key = np.take_along_axis(s[3::16] + np.float32(0.0), COL.reshape(8, C), axis=1).reshape(8, K, M)
    pile = np.take_along_axis(COL, np.argsort(-key, axis=2, kind="stable"), axis=2)
    sign = 4 * (s[0::16] > 0) + 2 * (s[1::16] > 0) + (s[2::16] > 0)
    k, h, used = np.arange(K), np.arange(K) % 8, np.zeros((8, K), np.int64)
    when = S * K + np.arange(C) + np.zeros((8, 1), np.int64)
    drawn = []
    for n in range(S):
        for i in range(7): h = np.where(used[h, k] == M, (h + 1) % 8, h)
        c = pile[h, k, used[h, k]]
        used[h, k] += 1
        when[h, c] = K * n + k
        drawn.append((h, c))
        h = sign[h, c]
    before = drawn[-1][1][CLOCK]
    for n in range(1, S): before[drawn[n]] = drawn[n - 1][1]
    q = np.argsort(when, axis=1, kind="stable")
    return q, np.take_along_axis(before, q, axis=1)
def reference(x, u, v, wc, ws):
    qu = [mx_ref.quantize(u[r]) for r in range(N)]
    lay = [pk(wc[r], ws[r]) for r in range(N)]
    now = [x[r] for r in range(N)]
    oq = np.zeros((N, 8, C), np.float32)
    for t in range(3):
        kept, blend = [], []
        for r in range(N):
            qx = mx_ref.quantize(now[r])
            q, p = walk(mx_ref.matmul(qu[r], qx))
            own = decode(qx).astype(BF)
            a = gcols(own, q).astype(np.float32)
            kept.append(a)
            blend.append(mx_ref.quantize(((a + gcols(own, p).astype(np.float32)) * np.float32(0.5)).astype(BF)))
            oq[r] = q
        new = []
        for r in range(N):
            m = join(pick(blend[r ^ PARTNER[t]], np.arange(H)), pick(blend[r], np.arange(H, C)))
            new.append(tile([(mx_ref.matmul(pick(lay[r], np.arange(128 * b, 128 * b + 128)), m) * np.float32(0.0009765625) + kept[r][:, b::4]) * np.float32(0.5) for b in range(4)]))
        now = new
    y = np.zeros((N, 128, C), np.float32)
    oc, osc = np.zeros((N, 128, 4 * C), np.uint8), np.zeros((N, 16, C), np.uint8)
    for r in range(N):
        qx = mx_ref.quantize(now[r])
        y[r] = mx_ref.matmul(mx_ref.quantize(v[r]), qx)
        oc[r], osc[r] = emit(qx)
    return {"y": y, "oq": oq, "oc": oc, "osc": osc}

@@ -1,0 +1,452 @@
+import numpy as np
+from concourse.mybir import dt, AluOpType as Op, ActivationFunctionType as AF
+
+F, B, I, U16 = "float32", "bfloat16", "int32", "uint16"
+C8, U8 = "float8_e4m3fn_x4", "uint8"
+
+
+def _sb(t, *s):
+    return ("sbuf", [128] + list(s), t)
+
+
+SCRATCH = {
+    "xin": _sb(B, 64, 20), "xt": _sb(B, 5, 64, 4), "xl": _sb(B, 1280), "ut": _sb(B, 512), "vt": _sb(B, 512),
+    "xq": _sb(C8, 384), "xs": _sb(U8, 384), "uq": _sb(C8, 128), "us": _sb(U8, 128), "vq": _sb(C8, 128), "vs": _sb(U8, 128),
+    "wq": _sb(C8, 512), "wsc": _sb(U8, 512), "lq": _sb(C8, 320), "lsc": _sb(U8, 320),
+    "sc": _sb(F, 32, 5), "cm": _sb(F, 4, 8, 5), "a2": _sb(F, 2, 8, 5), "rk": _sb(F, 40), "pb": _sb(F, 3, 8, 5),
+    "pac": _sb(F, 40), "pad": _sb(F, 40), "pay": _sb(F, 41), "d1": _sb(F, 40), "ne1": _sb(F, 5, 40), "prb": _sb(F, 40, 5),
+    "rt": _sb(B, 26, 5, 4), "rq": _sb(C8, 168), "rs": _sb(U8, 168),
+    "tb": _sb(F, 51), "dtb": _sb(F, 50), "val": _sb(F, 50), "al": _sb(F, 50), "eq": _sb(F, 50), "am": _sb(F, 50), "so": _sb(F, 14, 50),
+    "hi": _sb(F, 14), "fr": _sb(F, 14), "phi": _sb(F, 14), "cde": _sb(I, 64), "ca": _sb(I, 64), "pt": _sb(B, 512),
+    "ptq": _sb(C8, 192), "pts": _sb(U8, 192), "nei": _sb(F, 5, 64), "pc": _sb(F, 65), "dp": _sb(F, 64), "uop": _sb(F, 5, 64),
+    "fl": _sb(F, 20), "flm": _sb(F, 20), "inc": _sb(F, 20), "pr": _sb(F, 20), "pk": _sb(F, 65),
+    "v2": _sb(F, 40), "vm": _sb(F, 2, 5, 4, 4), "dg": _sb(B, 512), "dgq": _sb(C8, 168), "dgs": _sb(U8, 168),
+    "ofp": _sb(U16, 20), "ofq": _sb(U16, 20), "row": _sb(F, 400),
+    "tr": _sb(F, 5, 2, 64), "trl": _sb(F, 2, 320), "te": _sb(F, 20), "to": _sb(F, 20), "off": _sb(U16, 20),
+    "tp": _sb(B, 1280), "tw": _sb(B, 1280), "zp": _sb(B, 1280), "zt": _sb(B, 1280), "at": _sb(B, 1280), "tm": _sb(F, 8, 160), "yb": _sb(F, 320),
+    "zz": _sb(B, 512), "iw": _sb(I, 160, 4), "wm01": _sb(B, 160, 4), "wat": _sb(B, 160, 4), "wbt": _sb(B, 160, 4),
+    "waq": _sb(C8, 160), "was": _sb(U8, 160), "wbq": _sb(C8, 160), "wbs": _sb(U8, 160),
+    "et": _sb(B, 516), "ones": _sb(B, 128), "eqc": _sb(C8, 512), "eqs": _sb(U8, 512),
+    "wmt": _sb(B, 128, 4), "wut": _sb(B, 128, 4), "wrt": _sb(B, 128, 4),
+    "cq3": _sb(C8, 384), "cs3": _sb(U8, 384),
+    "ik": _sb(I, 64), "nr": _sb(I, 64, 4), "jr": _sb(I, 16, 4),
+    "n40": _sb(I, 40), "nb40": _sb(I, 40), "msk": _sb(F, 4, 40), "ngf": _sb(F, 4), "ngm": _sb(F, 4),
+    "cti": _sb(I, 50), "ct": _sb(F, 50), "val0": _sb(F, 50),
+    "pi": _sb(I, 8), "s0": _sb(F, 2), "me": _sb(F, 2), "mo": _sb(F, 2), "cqo": _sb(F, 2),
+    "ci2": _sb(F, 40), "cqc": _sb(F, 65), "mk": _sb(F, 64), "one5": _sb(F, 8), "cf4": _sb(F, 8), "phr": _sb(F, 320), "lgr": _sb(F, 320),
+}
+for _k in ("send", "stay", "land"):
+    SCRATCH[_k + "c"] = _sb(C8, 480)
+    SCRATCH[_k + "p"] = _sb(U8, 480)
+for _t in range(8):
+    SCRATCH["ps%d" % _t] = ("psum", [128, 512], F)
+SEMAPHORES = ["v", "s", "t", "p", "dx", "du", "dw", "dv", "fin"] + ["%s%d" % (a, i) for a in ("arr", "snd") for i in range(3)]
+
+M1 = 12582912.0
+PARTNER = [1, 2, 3]
+
+
+def rank_program(g, core, T, topo):
+    rank = T.rank_of(core)
+    if rank is None:
+        return
+    queue = {"v": g.vector, "s": g.scalar, "t": g.tensor, "p": g, "y": g.sync}
+    count, known, last, reads = {}, {e: {} for e in queue}, {}, {}
+
+    def need(e, sem, val):
+        if known[e].get(sem, 0) < val:
+            queue[e].wait_ge(T.sem[sem], val)
+            known[e][sem] = val
+
+    def pre(e, rd, wr):
+        for k in rd.split():
+            for s, n in last.get(k, {}).items():
+                need(e, s, n)
+        for k in wr.split():
+            for s, n in list(last.get(k, {}).items()) + list(reads.get(k, {}).items()):
+                need(e, s, n)
+
+    def post(sem, n, rd, wr, more=False):
+        count[sem] = count.get(sem, 0) + n
+        for k in rd.split():
+            reads.setdefault(k, {})[sem] = count[sem]
+        for k in wr.split():
+            old = last.get(k, {}) if more else {}
+            last[k] = {**old, sem: count[sem]}
+            if not more:
+                reads[k] = {}
+
+    def do(e, rd, wr, call, sem=None, n=1, more=False):
+        pre(e, rd, "" if more else wr)
+        if e == "p":
+            need("p", "p", count.get("p", 0))
+        if more:
+            for k in wr.split():
+                for s, c in reads.get(k, {}).items():
+                    if s != e:
+                        need(e, s, c)
+        sem = sem or e
+        call().then_inc(T.sem[sem], n)
+        post(sem, n, rd, wr, more)
+
+    V, S, P, Y = g.vector, g.scalar, g, g.sync
+
+    def tt(wr, rd, out, a, b, op, more=False):
+        do("v", rd, wr, lambda: V.tensor_tensor(out, a, b, op), more=more)
+
+    def ts(wr, rd, out, a, s1, op0, s2=None, op1=None, more=False):
+        if op1 is None:
+            do("v", rd, wr, lambda: V.tensor_scalar(out, a, s1, None, op0), more=more)
+        else:
+            do("v", rd, wr, lambda: V.tensor_scalar(out, a, s1, s2, op0, op1), more=more)
+
+    def scan(wr, rd, out, a, b, more=False, initial=0.0):
+        do("v", rd, wr, lambda: V.tensor_tensor_scan(out, a, b, initial, Op.mult, Op.add), more=more)
+
+    def copy(wr, rd, out, a, more=False):
+        do("v", rd, wr, lambda: V.tensor_copy(out, a), more=more)
+
+    def fill(wr, out, c, more=False):
+        do("v", "", wr, lambda: V.memset(out, c), more=more)
+
+    def quant(wr, rd, q, s, t, more=False):
+        do("v", rd, wr, lambda: V.quantize_mx(q, s, t), more=more)
+
+    def act(wr, rd, out, a, scale=None, more=False, bias=None):
+        if bias is not None:
+            do("s", rd, wr, lambda: S.activation(out, a, AF.Identity, bias=bias), more=more)
+        elif scale is None:
+            do("s", rd, wr, lambda: S.activation(out, a, AF.Copy), more=more)
+        else:
+            do("s", rd, wr, lambda: S.activation(out, a, AF.Copy, scale=scale), more=more)
+
+    def iota(wr, out, pat, base, cm, more=False):
+        do("p", "", wr, lambda: P.iota(out, pat, base, cm), more=more)
+
+    def iotaf(wr, out, pat, base, cm):
+        do("p", "", wr, lambda: P.iota(out, pat, base, cm, allow_small_or_imprecise_dtypes=True))
+
+    def mm(wr, rd, *prods):
+        pre("t", rd, wr)
+        for i, p in enumerate(prods):
+            ins = g.tensor.matmul_mx(*p, i == 0, i == len(prods) - 1)
+        ins.then_inc(T.sem.t, 1)
+        post("t", 1, rd, wr)
+
+    do("y", "", "xin", lambda: Y.dma_start(T.xin[:], T.x[:]), "dx", 16)
+    for G in range(8):
+        gg = 7 - G
+        q = ("s", S) if G % 2 else ("y", Y)
+        do(q[0], "", "ut", lambda: q[1].dma_start(T.ut[:, 16 * G:16 * G + 16], T.u[:, 64 * gg:64 * gg + 16]), "du", 16, more=True)
+    do("s", "", "ut", lambda: S.dma_start(T.ut[:, 128:512], T.u[:, 128:512]), "du", 16, more=True)
+    do("s", "", "wq", lambda: S.dma_start(T.wq[:].bitcast(dt.uint8), T.wc[:]), "dw", 16, more=True)
+    do("s", "", "wq", lambda: S.dma_start(T.wsc[:], T.ws[:]), "dw", 16, more=True)
+    do("y", "", "vt", lambda: Y.dma_start(T.vt[:], T.v[:]), "dv", 16)
+
+    lo, up = slice(0, 64), slice(64, 128)
+    iota("iw", T.iw[:], [[-1, 160], [8, 4]], -56, 1)
+    iota("cti", T.cti[:], [[-8, 10], [0, 5]], 72, 1)
+    iotaf("v0i", T.val0[:], [[-1, 50]], 49, 0)
+    iota("pi", T.pi[:, 0:4], [[0, 4]], 0, 1)
+    iotaf("ci2", T.ci2[:], [[0, 8], [1, 5]], -2, 0)
+    for h, sl in ((0, lo), (1, up)):
+        iota("n40", T.n40[sl, :], [[0, 10], [8, 4]], 32 * h, 1, more=True)
+        iota("nr", T.nr[sl, :, :], [[1, 64], [8, 4]], 32 * h, 0, more=True)
+        iota("ik", T.ik[sl, :], [[-1, 64]], 0, 1, more=True)
+    iota("jr", T.jr[:], [[1, 16], [-8, 4]], 0, -1)
+    iotaf("phr", T.phr[:], [[1, 320]], 0, 0)
+    iotaf("lgr", T.lgr[:], [[1, 5], [5, 64]], 0, 0)
+
+    fill("zz", T.zz[:], 0.0)
+    fill("et0", T.et[:], 0.0)
+    fill("ones", T.ones[:], 1.0)
+    do("p", "ones et0", "et", lambda: P.affine_select(T.et[:, 3:515:4], T.ones[:], [[-1, 128]], Op.is_equal, 0.0, 0, 1))
+    quant("xqz", "zz", T.xq[:, 256:384], T.xs[:, 256:384], T.zz[:])
+    quant("rqz", "zz", T.rq[:, 40:168], T.rs[:, 40:168], T.zz[:])
+    quant("ptqz", "zz", T.ptq[:, 64:192], T.pts[:, 64:192], T.zz[:])
+    quant("dgqz", "zz", T.dgq[:, 40:168], T.dgs[:, 40:168], T.zz[:])
+    fill("rt", T.rt[:], 0.0)
+    for i in range(5):
+        if i < 3:
+            copy("xt", "xin", T.xt[:, i, :, :], T.xin[:, :, 4 * i:4 * i + 4], more=True)
+        else:
+            act("xt", "xin", T.xt[:, i, :, :], T.xin[:, :, 4 * i:4 * i + 4], more=True)
+    quant("uq", "ut", T.uq[:], T.us[:], T.ut[:])
+    quant("xq", "xt xqz", T.xq[:, 0:320], T.xs[:, 0:320], T.xt[:])
+    fill("pay0", T.pay[:, 40:41], 0.0)
+    ts("iw2", "iw", T.iw[:], T.iw[:], 63, Op.bitwise_and)
+    ts("wm01", "iw2", T.wm01[lo], T.iw[lo], 0, Op.is_equal)
+    fill("wm01", T.wm01[up], 0.0, more=True)
+    act("wat", "wm01", T.wat[:], T.wm01[:], 0.625)
+    act("wbt", "wm01", T.wbt[:], T.wm01[:], -0.125)
+
+    def constants():
+        quant("wa", "wat", T.waq[:], T.was[:], T.wat[:])
+        quant("wb", "wbt", T.wbq[:], T.wbs[:], T.wbt[:])
+        for b in range(4):
+            quant("e%d" % b, "et", T.eqc[:, 128 * b:128 * b + 128], T.eqs[:, 128 * b:128 * b + 128], T.et[:, 3 - b:515 - b])
+        ts("cti2", "cti", T.cti[:], T.cti[:], 63, Op.bitwise_and)
+        ts("ct", "cti2", T.ct[:], T.cti[:], -1.0 / 512, Op.mult, 64.0625, Op.add)
+        ts("val0", "v0i", T.val0[:], T.val0[:], 64.4375, Op.add)
+        fill("tb0", T.tb[:, 50:51], 0.0)
+        ts("pj", "pi", T.pi[:, 4:6], T.pi[:, 0:2], 7, Op.bitwise_and)
+        ts("s0", "pj", T.s0[:], T.pi[:, 4:6], 5.0, Op.mult, 64.0, Op.add)
+
+    def constants2():
+        ts("pj2", "pi", T.pi[:, 6:8], T.pi[:, 0:2], 4, Op.logical_shift_right, 1, Op.bitwise_and)
+        copy("mo", "pj2", T.mo[:], T.pi[:, 6:8])
+        ts("me", "pj2", T.me[:], T.pi[:, 6:8], -1.0, Op.mult, 1.0, Op.add)
+        ts("cqo", "pj2", T.cqo[:, 0:1], T.pi[:, 6:7], 80.0, Op.mult, 160.0, Op.add)
+        ts("cqo", "pj2", T.cqo[:, 1:2], T.pi[:, 6:7], 16.0, Op.mult, 160.0, Op.add, more=True)
+        ts("nb40", "n40", T.nb40[:], T.n40[:], 63, Op.bitwise_and, 4, Op.logical_shift_right)
+        ts("n40b", "n40", T.n40[:], T.n40[:], 63, Op.bitwise_and)
+        copy("ngf", "n40b", T.ngf[:], T.n40[:, 0:4])
+        ts("ngm", "n40b", T.ngm[:], T.n40[:, 0:4], -160.0, Op.add)
+        for nb in range(4):
+            ts("msk", "nb40", T.msk[:, nb, :], T.nb40[:], nb, Op.is_equal, more=True)
+        fill("cqc1", T.cqc[:], -160.0)
+        for a in (slice(15, 64, 16), slice(64, 65)):
+            fill("cqc1", T.cqc[:, a], 0.0)
+        ts("cqc", "n40b cqc1", T.cqc[:, 0:64:16], T.n40[:, 0:4], 5.0, Op.mult, -160.0, Op.add)
+        fill("mk", T.mk[:], 1.0)
+        fill("mk", T.mk[:, 0:64:16], 0.0)
+        fill("mk", T.mk[:, 15:64:16], 0.0)
+        fill("one5", T.one5[:], 1.0)
+        fill("cf4", T.cf4[:, 0:4], 1024.0)
+        fill("cf4", T.cf4[:, 4:8], 0.0, more=True)
+        fill("code0", T.cde[:], 1)
+        fill("pc0", T.pc[:], 0.0)
+        fill("pk0", T.pk[:, 64:65], 0.0)
+        fill("pt0", T.pt[:], 0.0)
+        fill("dg0", T.dg[:], 0.0)
+        fill("row0", T.row[:], 0.0)
+        fill("wmz", T.wmt[:], 0.0)
+        fill("wuz", T.wut[:], 0.0)
+        fill("wrz", T.wrt[:], 0.0)
+        ts("nr2", "nr", T.nr[:], T.nr[:], 63, Op.bitwise_and)
+        ts("jr2", "jr", T.jr[:], T.jr[:], 15, Op.bitwise_and)
+        for h, sl in ((0, lo), (1, up)):
+            do("v", "wmz", "wmt", lambda: V.memset(T.wmt[sl, 64 * h:64 * h + 64, 1], 1.0), more=True)
+            ts("wmt", "ik wmz", T.wmt[sl, 64 * h:64 * h + 64, 0], T.ik[sl, :], 0, Op.is_ge, -1.0, Op.mult, more=True)
+            for t in range(4):
+                ts("wut", "nr2 ngf wuz", T.wut[sl, 64 * h:64 * h + 64, t], T.nr[sl, :, t], T.ngf[sl, t:t + 1], Op.is_le, more=True)
+                m = 64 * h + 16 * t
+                ts("wrt", "jr2 wrz", T.wrt[sl, m:m + 16, t], T.jr[sl, :, t], 0, Op.is_equal, more=True)
+        for j, k in enumerate(("wmt", "wut", "wrt")):
+            quant("q" + k, k, T.cq3[:, 128 * j:128 * j + 128], T.cs3[:, 128 * j:128 * j + 128], T[k][:])
+
+    def W3(j):
+        return T.cq3[:, 128 * j:128 * j + 128], T.cs3[:, 128 * j:128 * j + 128]
+
+    ps = [T["ps%d" % i] for i in range(8)]
+    partner_of = lambda t: T.cores[rank ^ PARTNER[t]]
+
+    for t in range(3):
+        final = t == 2
+        for i in range(5):
+            mm("ps%d" % i, "xq uq", (ps[i][:, 0:128], T.xq[:, 64 * i:64 * i + 128], T.xs[:, 64 * i:64 * i + 128], T.uq[:], T.us[:]))
+        if t == 0:
+            constants()
+        for i in range(5):
+            if i % 2:
+                act("sc", "ps%d" % i, T.sc[:, :, i], ps[i][:, 0:32], more=i > 0)
+            else:
+                copy("sc", "ps%d" % i, T.sc[:, :, i], ps[i][:, 0:32], more=i > 0)
+        for b, k in enumerate((5, 6, 7, 0)):
+            mm("ps%d" % k, "xq e%d" % b, (ps[k][:, 0:320], T.eqc[:, 128 * b:128 * b + 128], T.eqs[:, 128 * b:128 * b + 128], T.xq[:, 0:320], T.xs[:, 0:320]))
+            act("tp", "ps%d" % k, T.tp[:, 320 * b:320 * b + 320], ps[k][:, 0:320], 0.5, more=b > 0)
+        act("tw", "tp", T.tw[:], T.tp[:])
+        key = lambda a, b: T.sc[:, 3:32:4, a:b]
+        for s in range(1, 5):
+            tt("cm", "sc", T.cm[:, s - 1, :, 0:5 - s], key(s, 5), key(0, 5 - s), Op.is_gt, more=True)
+            tt("cm", "sc", T.cm[:, s - 1, :, 5 - s:5], key(0, s), key(5 - s, 5), Op.is_ge, more=True)
+        for b in range(3):
+            ts("pb%d" % b, "sc", T.pb[:, b, :, :], T.sc[:, b:32:4, :], 0.0, Op.is_gt, 32.0 / 2 ** b, Op.mult)
+        tt("a2", "cm", T.a2[:], T.cm[:, 0:2, :, :], T.cm[:, 2:4, :, :], Op.add)
+        tt("pac", "pb0 pb1", T.pac[:], T.pb[:, 0, :, :], T.pb[:, 1, :, :], Op.add)
+        tt("pad", "pb2 ci2", T.pad[:], T.pb[:, 2, :, :], T.ci2[:], Op.add)
+        tt("rk", "a2", T.rk[:], T.a2[:, 0, :, :], T.a2[:, 1, :, :], Op.add)
+        tt("pay", "pac pad", T.pay[:, 0:40], T.pac[:], T.pad[:], Op.add)
+        for r in range(3):
+            ts("ne1%d" % r, "rk", T.ne1[:, r, :], T.rk[:], 4.0 - r, Op.not_equal)
+        tt("d1a", "pay pay0", T.d1[:], T.pay[:, 0:40], T.pay[:, 1:41], Op.subtract)
+        for r in range(3, 5):
+            ts("ne1%d" % r, "rk", T.ne1[:, r, :], T.rk[:], 4.0 - r, Op.not_equal)
+        copy("d1", "pay d1a", T.d1[:, 4:40:5], T.pay[:, 4:40:5])
+        for r in range(5):
+            scan("prb", "ne1%d d1" % r, T.prb[:, :, r], T.ne1[:, r, :], T.d1[:], more=True)
+        for e in range(4):
+            ts("rth%d" % e, "prb rt", T.rt[:, e:8:4, :, e], T.prb[:, 4 + 5 * e:40:20, :], M1 * 8, Op.add, M1 * 8, Op.subtract)
+        for e in range(4):
+            tt("rtl%d" % e, "prb rth%d" % e, T.rt[:, 8 + e:16:4, :, e], T.prb[:, 4 + 5 * e:40:20, :], T.rt[:, e:8:4, :, e], Op.subtract)
+        quant("rq", "rqz rth0 rth1 rth2 rth3 rtl0 rtl1 rtl2 rtl3", T.rq[:, 0:130], T.rs[:, 0:130], T.rt[:])
+        for k, w in ((1, 0), (2, 32)):
+            mm("ps%d" % k, "wa wb rq rqz",
+               (ps[k][:, 0:128], T.waq[:, w:w + 128], T.was[:, w:w + 128], T.rq[:, 0:128], T.rs[:, 0:128]),
+               (ps[k][:, 0:128], T.wbq[:, w:w + 128], T.wbs[:, w:w + 128], T.rq[:, 40:168], T.rs[:, 40:168]))
+        tt("tb1", "ps1 ct", T.tb[:, 10:30], ps[1][:, 0:20], T.ct[:, 10:30], Op.add)
+        tt("tb2", "ps2 ct", T.tb[:, 30:50], ps[2][:, 20:40], T.ct[:, 30:50], Op.add)
+        tt("tb3", "ps2 ct", T.tb[:, 0:10], ps[2][:, 30:40], T.ct[:, 0:10], Op.add)
+        ts("am", "val0 s0", T.am[:], T.val0[:], T.s0[:, 0:1], Op.is_lt)
+        tt("dtb", "tb1 tb2 tb3 tb0", T.dtb[:], T.tb[:, 0:50], T.tb[:, 1:51], Op.subtract)
+        scan("so0", "am dtb", T.so[:, 0, :], T.am[:], T.dtb[:])
+        for n in range(1, 14):
+            s, so = T.so[:, n - 1, 49:50], "so%d" % (n - 1)
+            vk, vv = ("val0", T.val0) if n == 1 else ("val", T.val)
+            ts("al", vk + " " + so, T.al[:], vv[:], s, Op.is_lt)
+            ts("eq", so, T.eq[:], T.tb[:, 0:50], s, Op.is_equal, 64.0, Op.mult)
+            tt("am", "al eq", T.am[:], T.al[:], T.eq[:], Op.not_equal)
+            if n < 13:
+                tt("val", vk + " eq", T.val[:], vv[:], T.eq[:], Op.subtract)
+            scan("so%d" % n, "am dtb", T.so[:, n, :], T.am[:], T.dtb[:])
+        if t == 0:
+            constants2()
+        y = T.so[:, :, 49]
+        ts("hi", "so0 so13", T.hi[:], y, M1, Op.add, M1, Op.subtract)
+        tt("fr", "hi", T.fr[:], y, T.hi[:], Op.subtract)
+        for e in range(4):
+            ts("code%d" % e, "fr ngm code0", T.cde[:, 16 * e + 1:16 * e + 15], T.fr[:], -512.0, Op.mult, T.ngm[:, e:e + 1], Op.subtract)
+        ts("phi", "fr", T.phi[:], T.fr[:], -512.0, Op.mult)
+        codes = "code0 code1 code2 code3"
+        ts("ca", codes, T.ca[:], T.cde[:], 63, Op.bitwise_and)
+        for e in range(4):
+            act("pc", "phi pc0", T.pc[:, 16 * e + 2:16 * e + 15], T.phi[:, 0:13], more=e > 0)
+        act("pc", "phi cf4", T.pc[:, 0:64:16], T.cf4[:, 0:4], bias=T.phi[:, 13:14], more=True)
+        act("pc", "phi cf4", T.pc[:, 1:64:16], T.cf4[:, 4:8], bias=T.phi[:, 13:14], more=True)
+        ts("pto", "ca pt0", T.pt[:, 0:256:4], T.ca[:], 0, Op.is_equal)
+        for i in range(2):
+            ts("nea", codes, T.nei[:, i, :], T.cde[:], 64.0 * i, Op.not_equal, more=True)
+        scan("pti", "mk pto", T.pt[:, 1:256:4], T.mk[:], T.pt[:, 0:256:4])
+        for i in range(2, 4):
+            ts("nea", codes, T.nei[:, i, :], T.cde[:], 64.0 * i, Op.not_equal, more=True)
+        copy("ptu", "pti", T.pt[:, 256:452:65], T.pt[:, 57:256:64])
+        ts("nea", codes, T.nei[:, 4, :], T.cde[:], 256.0, Op.not_equal, more=True)
+        quant("ptq", "pto pti ptu ptqz", T.ptq[:, 0:128], T.pts[:, 0:128], T.pt[:])
+        mm("ps3", "ptq ptqz qwmt qwut", (ps[3][:, 0:128], *W3(0), T.ptq[:, 0:128], T.pts[:, 0:128]),
+           (ps[3][:, 0:128], *W3(1), T.ptq[:, 64:192], T.pts[:, 64:192]))
+        do("v", "nea", "nei", lambda: V.memset(T.nei[:, :, 0:64:16], 0.0))
+        tt("dp", "pc pc0", T.dp[:], T.pc[:, 0:64], T.pc[:, 1:65], Op.subtract)
+        for i in range(5):
+            scan("uop", "nei dp", T.uop[:, i, :], T.nei[:, i, :], T.dp[:], more=True)
+        up5 = T.uop[:, :, 14:64:16]
+        ts("fl", "uop", T.fl[:], up5, 512.0, Op.is_ge)
+        ts("flm", "uop", T.flm[:], up5, 512.0, Op.is_ge, -1024.0, Op.mult)
+        for e in range(4):
+            scan("inc", "fl one5", T.inc[:, e:20:4], T.one5[:, 0:5], T.fl[:, e:20:4], more=True, initial=-1.0)
+        tt("v2p", "uop flm", T.v2[:, 0:20], up5, T.flm[:], Op.add)
+        tt("pr", "fl inc", T.pr[:], T.fl[:], T.inc[:], Op.mult)
+        tt("pk", "ps3 cqc", T.pk[:, 0:64], ps[3][:, 0:64], T.cqc[:, 0:64], Op.add)
+        tt("dp", "pk pk0", T.dp[:], T.pk[:, 0:64], T.pk[:, 1:65], Op.subtract)
+        for i in range(5):
+            scan("uop", "nei dp", T.uop[:, i, :], T.nei[:, i, :], T.dp[:], more=i > 0)
+        tt("v2q", "uop pr", T.v2[:, 20:40], up5, T.pr[:], Op.add)
+        for nb in range(4):
+            tt("vm", "v2p v2q msk", T.vm[:, :, :, nb, :], T.v2[:], T.msk[:, nb, :], Op.mult, more=True)
+        ts("dgh", "vm dg0", T.dg[:, 160:320], T.vm[:], M1 * 32, Op.add, M1 * 32, Op.subtract)
+        tt("dgl", "vm dgh", T.dg[:, 0:160], T.vm[:], T.dg[:, 160:320], Op.subtract)
+        quant("dgq", "dgh dgl dgqz", T.dgq[:, 0:128], T.dgs[:, 0:128], T.dg[:])
+        mm("ps4", "dgq dgqz qwrt", (ps[4][:, 0:128], *W3(2), T.dgq[:, 0:128], T.dgs[:, 0:128]),
+           (ps[4][:, 0:128], *W3(2), T.dgq[:, 40:168], T.dgs[:, 40:168]))
+        ci = 1 if final else 0
+        ts("ofq", "ps4 cqo", T.ofq[:], ps[4][:, 20:40], T.cqo[:, ci:ci + 1], Op.add)
+        ts("ofp", "ps4", T.ofp[:], ps[4][:, 0:20], 160.0, Op.add)
+        do("v", "ofq phr row0", "row", lambda: V.tensor_copy(T.row[:].indirect(T.ofq[:, 0:20]), T.phr[:]))
+        for b in range(4):
+            cs = slice(320 * b, 320 * b + 320)
+            tt("zp%d" % b, "tp tw ofp", T.zp[:, cs], T.tw[:, cs].indirect(T.ofp[:, 0:20]), T.tp[:, cs], Op.add)
+        if final:
+            for a in range(2):
+                do("v", "row", "tr", lambda: V.transpose(T.trl[:, a, :], T.row[:, 16 * a:16 * a + 320]), more=a > 0)
+            for a in range(2):
+                ts("te%d" % a, "tr me", T.te[:, a:20:2], T.trl[:, a, 0:320:32], T.me[:, 0:1], Op.mult)
+                ts("to%d" % a, "tr mo", T.to[:, a:20:2], T.trl[:, a, 16:320:32], T.mo[:, 0:1], Op.mult)
+        else:
+            for i in range(5):
+                for a in range(2):
+                    c = i + 80 * a
+                    do("v", "row", "tr", lambda: V.transpose(T.tr[:, i, a, :], T.row[:, c:c + 316:5]), more=i + a > 0)
+            for h in range(2):
+                sl = slice(10 * h, 10 * h + 10)
+                ts("te%d" % h, "tr me", T.te[:, sl], T.tr[:, :, :, 32 * h], T.me[:, 0:1], Op.mult)
+                ts("to%d" % h, "tr mo", T.to[:, sl], T.tr[:, :, :, 32 * h + 16], T.mo[:, 0:1], Op.mult)
+        tt("ql", "te0 te1 to0 to1", T.to[:], T.te[:], T.to[:], Op.add)
+        copy("off0", "ql", T.off[:], T.to[:])
+
+        def picks(h):
+            o, cs = T.off[:, 10 * h:10 * h + 10], slice(640 * h, 640 * h + 640)
+            for b in range(2):
+                do("v", "off0 zp%d" % b, "zt%d" % h, lambda: V.tensor_copy(T.zt[:, 640 * h + b:640 * h + 640:4], T.zp[:, 320 * b:320 * b + 320].indirect(o)), more=b > 0)
+            for b in range(2, 4):
+                act("zt%d" % h, "off0 zp%d" % b, T.zt[:, 640 * h + b:640 * h + 640:4], T.zp[:, 320 * b:320 * b + 320].indirect(o), more=True)
+            return cs
+
+        def kept(h, b, e):
+            o = T.off[:, 10 * h:10 * h + 10]
+            out, win = T.at[:, 640 * h + b:640 * h + 640:4], T.tp[:, 320 * b:320 * b + 320].indirect(o)
+            if e == "v":
+                ts("at%d%d" % (h, b), "off0 tp", out, win, 2048.0, Op.mult)
+            else:
+                act("at%d%d" % (h, b), "off0 tp", out, win, 2048.0)
+
+        def new(h, b, k, cod):
+            mm("ps%d" % k, "wq " + cod[0], (ps[k][:, 0:160], T.wq[:, 128 * b:128 * b + 128], T.wsc[:, 128 * b:128 * b + 128], cod[1], cod[2]))
+
+        def finish(h, b, k):
+            tt("tm%d%d" % (h, b), "ps%d at%d%d" % (k, h, b), T.tm[:, 4 * h + b, :], ps[k][:, 0:160], T.at[:, 640 * h + b:640 * h + 640:4], Op.add)
+            if final:
+                act("xl%d" % h, "tm%d%d" % (h, b), T.xl[:, 640 * h + b:640 * h + 640:4], T.tm[:, 4 * h + b, :], 2.0 ** -11, more=b > 0)
+            else:
+                act("xt", "tm%d%d" % (h, b), T.xt[:, :, 32 * h:32 * h + 32, b], T.tm[:, 4 * h + b, :], 2.0 ** -11, more=h == 0 or b > 0)
+
+        rc = slice(160 * t, 160 * t + 160)
+        cs = picks(0)
+        quant("sq%d" % t, "zt0", T.sendc[:, rc], T.sendp[:, rc], T.zt[:, cs])
+        dst = partner_of(t)
+        rid, pid, _ = topo.addr(dst)
+        pre("p", "sq%d" % t, "")
+        for a, b in ((T.landc[:, rc].bitcast(dt.uint8), T.sendc[:, rc].bitcast(dt.uint8)), (T.landp[:, rc], T.sendp[:, rc])):
+            g.remote_dma(a, b, T.sem["arr%d" % t], T.sem["snd%d" % t], pid, rid, topo.mask(core, dst))
+        eng = 2 * len(topo.engines(core, dst))
+        last["land%d" % t] = {"arr%d" % t: eng}
+        cs = picks(1)
+        quant("stay%d" % t, "zt1", T.stayc[:, rc], T.stayp[:, rc], T.zt[:, cs])
+        for b in range(4):
+            new(1, b, 4 + b, ("stay%d" % t, T.stayc[:, rc], T.stayp[:, rc]))
+        for h in (1, 0):
+            for b in range(4):
+                kept(h, b, "v" if b < 2 else "s")
+            if h:
+                for b in range(4):
+                    finish(1, b, 4 + b)
+        if t == 0:
+            quant("vq", "vt", T.vq[:], T.vs[:], T.vt[:])
+        if final:
+            quant("lq1", "xl1", T.lq[:, 160:320], T.lsc[:, 160:320], T.xl[:, 640:1280])
+            do("v", "ofq lgr row0", "row", lambda: V.tensor_copy(T.row[:].indirect(T.ofq[:, 0:20]), T.lgr[:]))
+            mm("ps4", "lq1 vq", (ps[4][:, 0:160], T.vq[:], T.vs[:], T.lq[:, 160:320], T.lsc[:, 160:320]))
+            do("y", "row", "", lambda: Y.dma_start(T.oq[0:8:2, :], T.row[0:128:32, 0:320]), "fin", 16)
+            do("y", "row", "", lambda: Y.dma_start(T.oq[1:8:2, :], T.row[16:128:32, 16:336]), "fin", 16)
+            do("y", "lq1", "", lambda: Y.dma_start(T.oc[:, 640:1280], T.lq[:, 160:320].bitcast(dt.uint8)), "fin", 16)
+            copy("yb1", "ps4", T.yb[:, 160:320], ps[4][:, 0:160])
+            do("y", "yb1", "", lambda: Y.dma_start(T.y[:, 160:320], T.yb[:, 160:320]), "fin", 16)
+        for b in range(4):
+            new(0, b, b, ("land%d" % t, T.landc[:, rc], T.landp[:, rc]))
+        for b in range(4):
+            finish(0, b, b)
+        need("p", "snd%d" % t, eng)
+        if not final:
+            quant("xq", "xt xqz", T.xq[:, 0:320], T.xs[:, 0:320], T.xt[:])
+
+    quant("lq0", "xl0", T.lq[:, 0:160], T.lsc[:, 0:160], T.xl[:, 0:640])
+    mm("ps5", "lq0 vq", (ps[5][:, 0:160], T.vq[:], T.vs[:], T.lq[:, 0:160], T.lsc[:, 0:160]))
+    do("y", "lq0", "", lambda: Y.dma_start(T.oc[:, 0:640], T.lq[:, 0:160].bitcast(dt.uint8)), "fin", 16)
+    for k in range(4):
+        q = ("s", S) if k % 2 else ("y", Y)
+        do(q[0], "lq0 lq1", "", lambda: q[1].dma_start(T.osc[4 * k:4 * k + 4, :], T.lsc[32 * k:32 * k + 4, :]), "fin", 16)
+    copy("yb0", "ps5", T.yb[:, 0:160], ps[5][:, 0:160])
+    do("y", "yb0", "", lambda: Y.dma_start(T.y[:, 0:160], T.yb[:, 0:160]), "fin", 16)
+    need("y", "fin", count["fin"])
+    for k in ("v", "s", "t", "p"):
+        need("y", k, count[k])
+    for k in ("dx", "du", "dw", "dv"):
+        need("y", k, count[k])

@@ -16,18 +16,18 @@ SCRATCH = {
     "sc": _sb(F, 32, 5), "cm": _sb(F, 4, 8, 5), "a2": _sb(F, 2, 8, 5), "rk": _sb(F, 40), "pb": _sb(F, 3, 8, 5),
     "pac": _sb(F, 40), "pad": _sb(F, 40), "pay": _sb(F, 41), "d1": _sb(F, 40), "ne1": _sb(F, 5, 40), "prb": _sb(F, 40, 5),
     "rt": _sb(B, 26, 5, 4), "rq": _sb(C8, 168), "rs": _sb(U8, 168),
-    "tb": _sb(F, 51), "dtb": _sb(F, 50), "val": _sb(F, 50), "al": _sb(F, 50), "eq": _sb(F, 50), "am": _sb(F, 50), "so": _sb(F, 14, 50),
-    "hi": _sb(F, 14), "fr": _sb(F, 14), "phi": _sb(F, 14), "cde": _sb(I, 64), "ca": _sb(I, 64), "pt": _sb(B, 512),
+    "tb": _sb(F, 51), "tbb": _sb(F, 50), "val": _sb(F, 50), "eq": _sb(F, 50), "ab": _sb(F, 150), "dt3": _sb(F, 150), "so": _sb(F, 14, 150),
+    "phii": _sb(I, 14), "cdf": _sb(I, 64), "phi": _sb(F, 14), "cde": _sb(I, 64), "ca": _sb(I, 64), "pt": _sb(B, 512),
     "ptq": _sb(C8, 192), "pts": _sb(U8, 192), "nei": _sb(F, 5, 64), "pc": _sb(F, 65), "dp": _sb(F, 64), "uop": _sb(F, 5, 64),
     "fl": _sb(F, 20), "flm": _sb(F, 20), "inc": _sb(F, 20), "pr": _sb(F, 20), "pk": _sb(F, 65),
     "v2": _sb(F, 40), "vm": _sb(F, 2, 5, 4, 4), "dg": _sb(B, 512), "dgq": _sb(C8, 168), "dgs": _sb(U8, 168),
     "ofp": _sb(U16, 20), "ofq": _sb(U16, 20), "row": _sb(F, 400),
     "tr": _sb(F, 5, 2, 64), "trl": _sb(F, 2, 320), "te": _sb(F, 20), "to": _sb(F, 20), "off": _sb(U16, 20),
     "tp": _sb(B, 1280), "tw": _sb(B, 1280), "zp": _sb(B, 1280), "zt": _sb(B, 1280), "at": _sb(B, 1280), "tm": _sb(F, 8, 160), "yb": _sb(F, 320),
-    "zz": _sb(B, 512), "iw": _sb(I, 160, 4), "wm01": _sb(B, 160, 4), "wat": _sb(B, 160, 4), "wbt": _sb(B, 160, 4),
+    "zz": _sb(B, 512), "iw": _sb(I, 64, 4), "wm01": _sb(B, 64, 4), "wat": _sb(B, 160, 4), "wbt": _sb(B, 160, 4),
     "waq": _sb(C8, 160), "was": _sb(U8, 160), "wbq": _sb(C8, 160), "wbs": _sb(U8, 160),
     "et": _sb(B, 516), "ones": _sb(B, 128), "eqc": _sb(C8, 512), "eqs": _sb(U8, 512),
-    "wmt": _sb(B, 128, 4), "wut": _sb(B, 128, 4), "wrt": _sb(B, 128, 4),
+    "w3": _sb(B, 3, 128, 4),
     "cq3": _sb(C8, 384), "cs3": _sb(U8, 384),
     "ik": _sb(I, 64), "nr": _sb(I, 64, 4), "jr": _sb(I, 16, 4),
     "n40": _sb(I, 40), "nb40": _sb(I, 40), "msk": _sb(F, 4, 40), "ngf": _sb(F, 4), "ngm": _sb(F, 4),
@@ -43,6 +43,7 @@ for _t in range(8):
 SEMAPHORES = ["v", "s", "t", "p", "dx", "du", "dw", "dv", "fin"] + ["%s%d" % (a, i) for a in ("arr", "snd") for i in range(3)]
 
 M1 = 12582912.0
+EPS = 2.0 ** -30
 PARTNER = [1, 2, 3]
 
 
@@ -144,10 +145,13 @@ def rank_program(g, core, T, topo):
     do("y", "", "vt", lambda: Y.dma_start(T.vt[:], T.v[:]), "dv", 16)
 
     lo, up = slice(0, 64), slice(64, 128)
-    iota("iw", T.iw[:], [[-1, 160], [8, 4]], -56, 1)
+    iota("iw", T.iw[:], [[-1, 64], [8, 4]], -56, 1)
     iota("cti", T.cti[:], [[-8, 10], [0, 5]], 72, 1)
-    iotaf("v0i", T.val0[:], [[-1, 50]], 49, 0)
     iota("pi", T.pi[:, 0:4], [[0, 4]], 0, 1)
+    fill("et0", T.et[:], 0.0)
+    fill("ones", T.ones[:], 1.0)
+    do("p", "ones et0", "et", lambda: P.affine_select(T.et[:, 3:515:4], T.ones[:], [[-1, 128]], Op.is_equal, 0.0, 0, 1))
+    iotaf("v0i", T.val0[:], [[-1, 50]], 49, 0)
     iotaf("ci2", T.ci2[:], [[0, 8], [1, 5]], -2, 0)
     for h, sl in ((0, lo), (1, up)):
         iota("n40", T.n40[sl, :], [[0, 10], [8, 4]], 32 * h, 1, more=True)
@@ -158,14 +162,37 @@ def rank_program(g, core, T, topo):
     iotaf("lgr", T.lgr[:], [[1, 5], [5, 64]], 0, 0)
 
     fill("zz", T.zz[:], 0.0)
-    fill("et0", T.et[:], 0.0)
-    fill("ones", T.ones[:], 1.0)
-    do("p", "ones et0", "et", lambda: P.affine_select(T.et[:, 3:515:4], T.ones[:], [[-1, 128]], Op.is_equal, 0.0, 0, 1))
+    ts("iw2", "iw", T.iw[:], T.iw[:], 63, Op.bitwise_and)
+    fill("wm01", T.wm01[up], 0.0)
+    fill("rt", T.rt[:], 0.0)
+    ts("wm01", "iw2", T.wm01[lo], T.iw[lo], 0, Op.is_equal, more=True)
+    ts("cti2", "cti", T.cti[:], T.cti[:], 63, Op.bitwise_and)
+    ts("pj", "pi", T.pi[:, 4:6], T.pi[:, 0:2], 7, Op.bitwise_and)
+    for c, w in ((0, 64), (64, 64), (128, 32)):
+        act("wat", "wm01", T.wat[:, c:c + w, :], T.wm01[:, 0:w, :], 0.625, more=c > 0)
+        act("wbt", "wm01", T.wbt[:, c:c + w, :], T.wm01[:, 0:w, :], -0.125, more=c > 0)
     quant("xqz", "zz", T.xq[:, 256:384], T.xs[:, 256:384], T.zz[:])
     quant("rqz", "zz", T.rq[:, 40:168], T.rs[:, 40:168], T.zz[:])
     quant("ptqz", "zz", T.ptq[:, 64:192], T.pts[:, 64:192], T.zz[:])
     quant("dgqz", "zz", T.dgq[:, 40:168], T.dgs[:, 40:168], T.zz[:])
-    fill("rt", T.rt[:], 0.0)
+    ts("val0", "v0i", T.val0[:], T.val0[:], 64.4375, Op.add)
+    fill("pay0", T.pay[:, 40:41], 0.0)
+    fill("tb0", T.tb[:, 50:51], 0.0)
+    fill("abk", T.ab[:, 0:150:3], 1 / EPS)
+    fill("dt0", T.dt3[:], 0.0)
+    fill("cqc1", T.cqc[:], -160.0)
+    fill("mk", T.mk[:], 1.0)
+    fill("w3z", T.w3[:], 0.0)
+    fill("one5", T.one5[:], 1.0)
+    fill("code0", T.cde[:], 1)
+    fill("pc0", T.pc[:], 0.0)
+    fill("pk0", T.pk[:, 64:65], 0.0)
+    fill("cf4", T.cf4[:, 0:4], 1024.0)
+    fill("cf4", T.cf4[:, 4:8], 0.0, more=True)
+    for a in (slice(15, 64, 16), slice(64, 65)):
+        fill("cqc1", T.cqc[:, a], 0.0)
+    fill("mk", T.mk[:, 0:64:16], 0.0)
+    fill("mk", T.mk[:, 15:64:16], 0.0)
     for i in range(5):
         if i < 3:
             copy("xt", "xin", T.xt[:, i, :, :], T.xin[:, :, 4 * i:4 * i + 4], more=True)
@@ -173,67 +200,68 @@ def rank_program(g, core, T, topo):
             act("xt", "xin", T.xt[:, i, :, :], T.xin[:, :, 4 * i:4 * i + 4], more=True)
     quant("uq", "ut", T.uq[:], T.us[:], T.ut[:])
     quant("xq", "xt xqz", T.xq[:, 0:320], T.xs[:, 0:320], T.xt[:])
-    fill("pay0", T.pay[:, 40:41], 0.0)
-    ts("iw2", "iw", T.iw[:], T.iw[:], 63, Op.bitwise_and)
-    ts("wm01", "iw2", T.wm01[lo], T.iw[lo], 0, Op.is_equal)
-    fill("wm01", T.wm01[up], 0.0, more=True)
-    act("wat", "wm01", T.wat[:], T.wm01[:], 0.625)
-    act("wbt", "wm01", T.wbt[:], T.wm01[:], -0.125)
 
-    def constants():
+    def constants1():
         quant("wa", "wat", T.waq[:], T.was[:], T.wat[:])
         quant("wb", "wbt", T.wbq[:], T.wbs[:], T.wbt[:])
-        for b in range(4):
-            quant("e%d" % b, "et", T.eqc[:, 128 * b:128 * b + 128], T.eqs[:, 128 * b:128 * b + 128], T.et[:, 3 - b:515 - b])
-        ts("cti2", "cti", T.cti[:], T.cti[:], 63, Op.bitwise_and)
         ts("ct", "cti2", T.ct[:], T.cti[:], -1.0 / 512, Op.mult, 64.0625, Op.add)
-        ts("val0", "v0i", T.val0[:], T.val0[:], 64.4375, Op.add)
-        fill("tb0", T.tb[:, 50:51], 0.0)
-        ts("pj", "pi", T.pi[:, 4:6], T.pi[:, 0:2], 7, Op.bitwise_and)
         ts("s0", "pj", T.s0[:], T.pi[:, 4:6], 5.0, Op.mult, 64.0, Op.add)
 
     def constants2():
+        for b in range(4):
+            quant("e%d" % b, "et", T.eqc[:, 128 * b:128 * b + 128], T.eqs[:, 128 * b:128 * b + 128], T.et[:, 3 - b:515 - b])
+            yield
+        for k, a in (("pt0", T.pt), ("dg0", T.dg), ("row0", T.row)):
+            fill(k, a[:], 0.0)
+            yield
         ts("pj2", "pi", T.pi[:, 6:8], T.pi[:, 0:2], 4, Op.logical_shift_right, 1, Op.bitwise_and)
-        copy("mo", "pj2", T.mo[:], T.pi[:, 6:8])
-        ts("me", "pj2", T.me[:], T.pi[:, 6:8], -1.0, Op.mult, 1.0, Op.add)
-        ts("cqo", "pj2", T.cqo[:, 0:1], T.pi[:, 6:7], 80.0, Op.mult, 160.0, Op.add)
-        ts("cqo", "pj2", T.cqo[:, 1:2], T.pi[:, 6:7], 16.0, Op.mult, 160.0, Op.add, more=True)
+        yield
         ts("nb40", "n40", T.nb40[:], T.n40[:], 63, Op.bitwise_and, 4, Op.logical_shift_right)
+        yield
         ts("n40b", "n40", T.n40[:], T.n40[:], 63, Op.bitwise_and)
+        yield
+        ts("nr2", "nr", T.nr[:], T.nr[:], 63, Op.bitwise_and)
+        yield
+        yield
+        ts("jr2", "jr", T.jr[:], T.jr[:], 15, Op.bitwise_and)
+        yield
         copy("ngf", "n40b", T.ngf[:], T.n40[:, 0:4])
-        ts("ngm", "n40b", T.ngm[:], T.n40[:, 0:4], -160.0, Op.add)
+        yield
+        ts("ngm", "n40b", T.ngm[:], T.n40[:, 0:4], -1.0, Op.mult, 102560.0, Op.add)
+        yield
+        for h, sl in ((0, lo), (1, up)):
+            do("v", "w3z", "wt0", lambda: V.memset(T.w3[sl, 0, 64 * h:64 * h + 64, 1], 1.0), more=True)
+            yield
+            ts("wt0", "ik w3z", T.w3[sl, 0, 64 * h:64 * h + 64, 0], T.ik[sl, :], 0, Op.is_ge, -1.0, Op.mult, more=True)
+            yield
+            for t in range(4):
+                ts("wt1", "nr2 ngf w3z", T.w3[sl, 1, 64 * h:64 * h + 64, t], T.nr[sl, :, t], T.ngf[sl, t:t + 1], Op.is_le, more=True)
+                yield
+                m = 64 * h + 16 * t
+                ts("wt2", "jr2 w3z", T.w3[sl, 2, m:m + 16, t], T.jr[sl, :, t], 0, Op.is_equal, more=True)
+                yield
+        ts("cqc", "n40b cqc1", T.cqc[:, 0:64:16], T.n40[:, 0:4], 5.0, Op.mult, -160.0, Op.add)
+        yield
+        for j in range(3):
+            quant("qwt%d" % j, "wt%d" % j, T.cq3[:, 128 * j:128 * j + 128], T.cs3[:, 128 * j:128 * j + 128], T.w3[:, j, :, :])
+            yield
+            yield
         for nb in range(4):
             ts("msk", "nb40", T.msk[:, nb, :], T.nb40[:], nb, Op.is_equal, more=True)
-        fill("cqc1", T.cqc[:], -160.0)
-        for a in (slice(15, 64, 16), slice(64, 65)):
-            fill("cqc1", T.cqc[:, a], 0.0)
-        ts("cqc", "n40b cqc1", T.cqc[:, 0:64:16], T.n40[:, 0:4], 5.0, Op.mult, -160.0, Op.add)
-        fill("mk", T.mk[:], 1.0)
-        fill("mk", T.mk[:, 0:64:16], 0.0)
-        fill("mk", T.mk[:, 15:64:16], 0.0)
-        fill("one5", T.one5[:], 1.0)
-        fill("cf4", T.cf4[:, 0:4], 1024.0)
-        fill("cf4", T.cf4[:, 4:8], 0.0, more=True)
-        fill("code0", T.cde[:], 1)
-        fill("pc0", T.pc[:], 0.0)
-        fill("pk0", T.pk[:, 64:65], 0.0)
-        fill("pt0", T.pt[:], 0.0)
-        fill("dg0", T.dg[:], 0.0)
-        fill("row0", T.row[:], 0.0)
-        fill("wmz", T.wmt[:], 0.0)
-        fill("wuz", T.wut[:], 0.0)
-        fill("wrz", T.wrt[:], 0.0)
-        ts("nr2", "nr", T.nr[:], T.nr[:], 63, Op.bitwise_and)
-        ts("jr2", "jr", T.jr[:], T.jr[:], 15, Op.bitwise_and)
-        for h, sl in ((0, lo), (1, up)):
-            do("v", "wmz", "wmt", lambda: V.memset(T.wmt[sl, 64 * h:64 * h + 64, 1], 1.0), more=True)
-            ts("wmt", "ik wmz", T.wmt[sl, 64 * h:64 * h + 64, 0], T.ik[sl, :], 0, Op.is_ge, -1.0, Op.mult, more=True)
-            for t in range(4):
-                ts("wut", "nr2 ngf wuz", T.wut[sl, 64 * h:64 * h + 64, t], T.nr[sl, :, t], T.ngf[sl, t:t + 1], Op.is_le, more=True)
-                m = 64 * h + 16 * t
-                ts("wrt", "jr2 wrz", T.wrt[sl, m:m + 16, t], T.jr[sl, :, t], 0, Op.is_equal, more=True)
-        for j, k in enumerate(("wmt", "wut", "wrt")):
-            quant("q" + k, k, T.cq3[:, 128 * j:128 * j + 128], T.cs3[:, 128 * j:128 * j + 128], T[k][:])
+            yield
+        copy("mo", "pj2", T.mo[:], T.pi[:, 6:8])
+        yield
+        ts("me", "pj2", T.me[:], T.pi[:, 6:8], -1.0, Op.mult, 1.0, Op.add)
+        yield
+        ts("cqo", "pj2", T.cqo[:, 0:1], T.pi[:, 6:7], 80.0, Op.mult, 160.0, Op.add)
+        yield
+        ts("cqo", "pj2", T.cqo[:, 1:2], T.pi[:, 6:7], 16.0, Op.mult, 160.0, Op.add, more=True)
+
+    rest = constants2()
+
+    def fillers(n):
+        for _ in range(n):
+            next(rest, None)
 
     def W3(j):
         return T.cq3[:, 128 * j:128 * j + 128], T.cs3[:, 128 * j:128 * j + 128]
@@ -245,17 +273,19 @@ def rank_program(g, core, T, topo):
         final = t == 2
         for i in range(5):
             mm("ps%d" % i, "xq uq", (ps[i][:, 0:128], T.xq[:, 64 * i:64 * i + 128], T.xs[:, 64 * i:64 * i + 128], T.uq[:], T.us[:]))
-        if t == 0:
-            constants()
         for i in range(5):
             if i % 2:
                 act("sc", "ps%d" % i, T.sc[:, :, i], ps[i][:, 0:32], more=i > 0)
             else:
                 copy("sc", "ps%d" % i, T.sc[:, :, i], ps[i][:, 0:32], more=i > 0)
-        for b, k in enumerate((5, 6, 7, 0)):
-            mm("ps%d" % k, "xq e%d" % b, (ps[k][:, 0:320], T.eqc[:, 128 * b:128 * b + 128], T.eqs[:, 128 * b:128 * b + 128], T.xq[:, 0:320], T.xs[:, 0:320]))
-            act("tp", "ps%d" % k, T.tp[:, 320 * b:320 * b + 320], ps[k][:, 0:320], 0.5, more=b > 0)
-        act("tw", "tp", T.tw[:], T.tp[:])
+        def unpack():
+            for b, k in enumerate((5, 6, 7, 0)):
+                mm("ps%d" % k, "xq e%d" % b, (ps[k][:, 0:320], T.eqc[:, 128 * b:128 * b + 128], T.eqs[:, 128 * b:128 * b + 128], T.xq[:, 0:320], T.xs[:, 0:320]))
+                act("tp", "ps%d" % k, T.tp[:, 320 * b:320 * b + 320], ps[k][:, 0:320], 0.5, more=b > 0)
+            act("tw", "tp", T.tw[:], T.tp[:])
+
+        if t > 0:
+            unpack()
         key = lambda a, b: T.sc[:, 3:32:4, a:b]
         for s in range(1, 5):
             tt("cm", "sc", T.cm[:, s - 1, :, 0:5 - s], key(s, 5), key(0, 5 - s), Op.is_gt, more=True)
@@ -269,6 +299,8 @@ def rank_program(g, core, T, topo):
         tt("pay", "pac pad", T.pay[:, 0:40], T.pac[:], T.pad[:], Op.add)
         for r in range(3):
             ts("ne1%d" % r, "rk", T.ne1[:, r, :], T.rk[:], 4.0 - r, Op.not_equal)
+        if t == 0:
+            constants1()
         tt("d1a", "pay pay0", T.d1[:], T.pay[:, 0:40], T.pay[:, 1:41], Op.subtract)
         for r in range(3, 5):
             ts("ne1%d" % r, "rk", T.ne1[:, r, :], T.rk[:], 4.0 - r, Op.not_equal)
@@ -287,42 +319,50 @@ def rank_program(g, core, T, topo):
         tt("tb1", "ps1 ct", T.tb[:, 10:30], ps[1][:, 0:20], T.ct[:, 10:30], Op.add)
         tt("tb2", "ps2 ct", T.tb[:, 30:50], ps[2][:, 20:40], T.ct[:, 30:50], Op.add)
         tt("tb3", "ps2 ct", T.tb[:, 0:10], ps[2][:, 30:40], T.ct[:, 0:10], Op.add)
-        ts("am", "val0 s0", T.am[:], T.val0[:], T.s0[:, 0:1], Op.is_lt)
-        tt("dtb", "tb1 tb2 tb3 tb0", T.dtb[:], T.tb[:, 0:50], T.tb[:, 1:51], Op.subtract)
-        scan("so0", "am dtb", T.so[:, 0, :], T.am[:], T.dtb[:])
+        ts("aba", "val0 s0 abk", T.ab[:, 1:150:3], T.val0[:], T.s0[:, 0:1], Op.is_lt, EPS, Op.add)
+        fill("abb", T.ab[:, 2:150:3], EPS)
+        tt("dtb", "tb1 tb2 tb3 tb0 dt0", T.dt3[:, 2:150:3], T.tb[:, 0:50], T.tb[:, 1:51], Op.subtract)
+        tt("tbm", "val0 tb1 tb2 tb3", T.tbb[:], T.val0[:], T.tb[:, 0:50], Op.is_ge)
+        scan("so0", "aba abb dtb", T.so[:, 0, :], T.ab[:], T.dt3[:])
+        tt("tbb", "tbm", T.tbb[:], T.tbb[:], T.tb[:, 0:50], Op.mult)
         for n in range(1, 14):
-            s, so = T.so[:, n - 1, 49:50], "so%d" % (n - 1)
+            s, so = T.so[:, n - 1, 149:150], "so%d" % (n - 1)
             vk, vv = ("val0", T.val0) if n == 1 else ("val", T.val)
-            ts("al", vk + " " + so, T.al[:], vv[:], s, Op.is_lt)
-            ts("eq", so, T.eq[:], T.tb[:, 0:50], s, Op.is_equal, 64.0, Op.mult)
-            tt("am", "al eq", T.am[:], T.al[:], T.eq[:], Op.not_equal)
+            ts("aba", vk + " " + so, T.ab[:, 1:150:3], vv[:], s, Op.is_lt, EPS, Op.add)
+            ts("abb", "tbb " + so, T.ab[:, 2:150:3], T.tbb[:], s, Op.is_equal, EPS, Op.add)
+            if n < 13:
+                ts("eq", so, T.eq[:], T.tb[:, 0:50], s, Op.is_equal, 64.0, Op.mult)
+            fillers(2)
+            scan("so%d" % n, "aba abb dtb", T.so[:, n, :], T.ab[:], T.dt3[:])
             if n < 13:
                 tt("val", vk + " eq", T.val[:], vv[:], T.eq[:], Op.subtract)
-            scan("so%d" % n, "am dtb", T.so[:, n, :], T.am[:], T.dtb[:])
-        if t == 0:
-            constants2()
-        y = T.so[:, :, 49]
-        ts("hi", "so0 so13", T.hi[:], y, M1, Op.add, M1, Op.subtract)
-        tt("fr", "hi", T.fr[:], y, T.hi[:], Op.subtract)
+            fillers(2)
+            if t == 0 and n == 5:
+                unpack()
+        fillers(99)
+        y = T.so[:, :, 149]
         for e in range(4):
-            ts("code%d" % e, "fr ngm code0", T.cde[:, 16 * e + 1:16 * e + 15], T.fr[:], -512.0, Op.mult, T.ngm[:, e:e + 1], Op.subtract)
-        ts("phi", "fr", T.phi[:], T.fr[:], -512.0, Op.mult)
+            ts("code%d" % e, "so0 so13 ngm code0", T.cde[:, 16 * e + 1:16 * e + 15], y, -512.0, Op.mult, T.ngm[:, e:e + 1], Op.add)
+        ts("phii", "so13", T.phii[:], y, -512.0, Op.mult, 102560.0, Op.add)
         codes = "code0 code1 code2 code3"
         ts("ca", codes, T.ca[:], T.cde[:], 63, Op.bitwise_and)
+        ts("cdf", codes, T.cdf[:], T.cde[:], 511, Op.bitwise_and)
+        ts("phij", "phii", T.phii[:], T.phii[:], 511, Op.bitwise_and)
+        ts("pto", "ca pt0", T.pt[:, 0:256:4], T.ca[:], 0, Op.is_equal)
+        ts("phi", "phij", T.phi[:], T.phii[:], -160.0, Op.add)
         for e in range(4):
             act("pc", "phi pc0", T.pc[:, 16 * e + 2:16 * e + 15], T.phi[:, 0:13], more=e > 0)
         act("pc", "phi cf4", T.pc[:, 0:64:16], T.cf4[:, 0:4], bias=T.phi[:, 13:14], more=True)
         act("pc", "phi cf4", T.pc[:, 1:64:16], T.cf4[:, 4:8], bias=T.phi[:, 13:14], more=True)
-        ts("pto", "ca pt0", T.pt[:, 0:256:4], T.ca[:], 0, Op.is_equal)
         for i in range(2):
-            ts("nea", codes, T.nei[:, i, :], T.cde[:], 64.0 * i, Op.not_equal, more=True)
+            ts("nea", "cdf", T.nei[:, i, :], T.cdf[:], 64.0 * i, Op.not_equal, more=True)
         scan("pti", "mk pto", T.pt[:, 1:256:4], T.mk[:], T.pt[:, 0:256:4])
         for i in range(2, 4):
-            ts("nea", codes, T.nei[:, i, :], T.cde[:], 64.0 * i, Op.not_equal, more=True)
+            ts("nea", "cdf", T.nei[:, i, :], T.cdf[:], 64.0 * i, Op.not_equal, more=True)
         copy("ptu", "pti", T.pt[:, 256:452:65], T.pt[:, 57:256:64])
-        ts("nea", codes, T.nei[:, 4, :], T.cde[:], 256.0, Op.not_equal, more=True)
+        ts("nea", "cdf", T.nei[:, 4, :], T.cdf[:], 256.0, Op.not_equal, more=True)
         quant("ptq", "pto pti ptu ptqz", T.ptq[:, 0:128], T.pts[:, 0:128], T.pt[:])
-        mm("ps3", "ptq ptqz qwmt qwut", (ps[3][:, 0:128], *W3(0), T.ptq[:, 0:128], T.pts[:, 0:128]),
+        mm("ps3", "ptq ptqz qwt0 qwt1", (ps[3][:, 0:128], *W3(0), T.ptq[:, 0:128], T.pts[:, 0:128]),
            (ps[3][:, 0:128], *W3(1), T.ptq[:, 64:192], T.pts[:, 64:192]))
         do("v", "nea", "nei", lambda: V.memset(T.nei[:, :, 0:64:16], 0.0))
         tt("dp", "pc pc0", T.dp[:], T.pc[:, 0:64], T.pc[:, 1:65], Op.subtract)
@@ -345,7 +385,7 @@ def rank_program(g, core, T, topo):
         ts("dgh", "vm dg0", T.dg[:, 160:320], T.vm[:], M1 * 32, Op.add, M1 * 32, Op.subtract)
         tt("dgl", "vm dgh", T.dg[:, 0:160], T.vm[:], T.dg[:, 160:320], Op.subtract)
         quant("dgq", "dgh dgl dgqz", T.dgq[:, 0:128], T.dgs[:, 0:128], T.dg[:])
-        mm("ps4", "dgq dgqz qwrt", (ps[4][:, 0:128], *W3(2), T.dgq[:, 0:128], T.dgs[:, 0:128]),
+        mm("ps4", "dgq dgqz qwt2", (ps[4][:, 0:128], *W3(2), T.dgq[:, 0:128], T.dgs[:, 0:128]),
            (ps[4][:, 0:128], *W3(2), T.dgq[:, 40:168], T.dgs[:, 40:168]))
         ci = 1 if final else 0
         ts("ofq", "ps4 cqo", T.ofq[:], ps[4][:, 20:40], T.cqo[:, ci:ci + 1], Op.add)

@@ -16,11 +16,11 @@ SCRATCH = {
     "sc": _sb(F, 32, 5), "cm": _sb(F, 4, 8, 5), "a2": _sb(F, 2, 8, 5), "rk": _sb(F, 40), "pb": _sb(F, 3, 8, 5),
     "pac": _sb(F, 40), "pad": _sb(F, 40), "pay": _sb(F, 41), "d1": _sb(F, 40), "ne1": _sb(F, 5, 40), "prb": _sb(F, 40, 5),
     "rt": _sb(B, 26, 5, 4), "rq": _sb(C8, 168), "rs": _sb(U8, 168),
-    "tb": _sb(F, 51), "tbb": _sb(F, 50), "val": _sb(F, 50), "eq": _sb(F, 50), "ab": _sb(F, 150), "dt3": _sb(F, 150), "so": _sb(F, 14, 150),
+    "tb": _sb(F, 51), "tbb": _sb(F, 50), "val": _sb(F, 2, 50), "eq": _sb(F, 50), "ab": _sb(F, 150), "dt3": _sb(F, 150), "so": _sb(F, 14, 150),
     "phii": _sb(I, 14), "cdf": _sb(I, 64), "phi": _sb(F, 14), "cde": _sb(I, 64), "ca": _sb(I, 64), "pt": _sb(B, 512),
     "ptq": _sb(C8, 192), "pts": _sb(U8, 192), "nei": _sb(F, 5, 64), "pc": _sb(F, 65), "dp": _sb(F, 64), "uop": _sb(F, 5, 64),
     "fl": _sb(F, 20), "flm": _sb(F, 20), "inc": _sb(F, 20), "pr": _sb(F, 20), "pk": _sb(F, 65),
-    "v2": _sb(F, 40), "vm": _sb(F, 2, 5, 4, 4), "dg": _sb(B, 512), "dgq": _sb(C8, 168), "dgs": _sb(U8, 168),
+    "v2": _sb(F, 40), "vm": _sb(F, 2, 5, 4, 4), "dg": _sb(B, 1024), "dgq": _sb(C8, 336), "dgs": _sb(U8, 336),
     "ofp": _sb(U16, 20), "ofq": _sb(U16, 20), "row": _sb(F, 400),
     "tr": _sb(F, 5, 2, 64), "trl": _sb(F, 2, 320), "te": _sb(F, 20), "to": _sb(F, 20), "off": _sb(U16, 20),
     "tp": _sb(B, 1280), "tw": _sb(B, 1280), "zp": _sb(B, 1280), "zt": _sb(B, 1280), "at": _sb(B, 1280), "tm": _sb(F, 8, 160), "yb": _sb(F, 320),
@@ -33,7 +33,7 @@ SCRATCH = {
     "n40": _sb(I, 40), "nb40": _sb(I, 40), "msk": _sb(F, 4, 40), "ngf": _sb(F, 4), "ngm": _sb(F, 4),
     "cti": _sb(I, 50), "ct": _sb(F, 50), "val0": _sb(F, 50),
     "pi": _sb(I, 8), "s0": _sb(F, 2), "me": _sb(F, 2), "mo": _sb(F, 2), "cqo": _sb(F, 2),
-    "ci2": _sb(F, 40), "cqc": _sb(F, 65), "mk": _sb(F, 64), "one5": _sb(F, 8), "cf4": _sb(F, 8), "phr": _sb(F, 320), "lgr": _sb(F, 320),
+    "ci2": _sb(F, 40), "cqc": _sb(F, 65), "one5": _sb(F, 8), "cf4": _sb(F, 8), "phr": _sb(F, 320), "lgr": _sb(F, 320),
 }
 for _k in ("send", "stay", "land"):
     SCRATCH[_k + "c"] = _sb(C8, 480)
@@ -162,37 +162,10 @@ def rank_program(g, core, T, topo):
     iotaf("lgr", T.lgr[:], [[1, 5], [5, 64]], 0, 0)
 
     fill("zz", T.zz[:], 0.0)
-    ts("iw2", "iw", T.iw[:], T.iw[:], 63, Op.bitwise_and)
-    fill("wm01", T.wm01[up], 0.0)
-    fill("rt", T.rt[:], 0.0)
-    ts("wm01", "iw2", T.wm01[lo], T.iw[lo], 0, Op.is_equal, more=True)
-    ts("cti2", "cti", T.cti[:], T.cti[:], 63, Op.bitwise_and)
-    ts("pj", "pi", T.pi[:, 4:6], T.pi[:, 0:2], 7, Op.bitwise_and)
-    for c, w in ((0, 64), (64, 64), (128, 32)):
-        act("wat", "wm01", T.wat[:, c:c + w, :], T.wm01[:, 0:w, :], 0.625, more=c > 0)
-        act("wbt", "wm01", T.wbt[:, c:c + w, :], T.wm01[:, 0:w, :], -0.125, more=c > 0)
     quant("xqz", "zz", T.xq[:, 256:384], T.xs[:, 256:384], T.zz[:])
-    quant("rqz", "zz", T.rq[:, 40:168], T.rs[:, 40:168], T.zz[:])
-    quant("ptqz", "zz", T.ptq[:, 64:192], T.pts[:, 64:192], T.zz[:])
-    quant("dgqz", "zz", T.dgq[:, 40:168], T.dgs[:, 40:168], T.zz[:])
-    ts("val0", "v0i", T.val0[:], T.val0[:], 64.4375, Op.add)
-    fill("pay0", T.pay[:, 40:41], 0.0)
-    fill("tb0", T.tb[:, 50:51], 0.0)
-    fill("abk", T.ab[:, 0:150:3], 1 / EPS)
-    fill("dt0", T.dt3[:], 0.0)
-    fill("cqc1", T.cqc[:], -160.0)
-    fill("mk", T.mk[:], 1.0)
-    fill("w3z", T.w3[:], 0.0)
-    fill("one5", T.one5[:], 1.0)
-    fill("code0", T.cde[:], 1)
-    fill("pc0", T.pc[:], 0.0)
-    fill("pk0", T.pk[:, 64:65], 0.0)
-    fill("cf4", T.cf4[:, 0:4], 1024.0)
-    fill("cf4", T.cf4[:, 4:8], 0.0, more=True)
-    for a in (slice(15, 64, 16), slice(64, 65)):
-        fill("cqc1", T.cqc[:, a], 0.0)
-    fill("mk", T.mk[:, 0:64:16], 0.0)
-    fill("mk", T.mk[:, 15:64:16], 0.0)
+    act("rt", "zz", T.rt[:, 0:25, :, :], T.zz[:, 0:500])
+    act("rt", "zz", T.rt[:, 25, :, :], T.zz[:, 0:20], more=True)
+    act("pt0", "zz", T.pt[:], T.zz[:])
     for i in range(5):
         if i < 3:
             copy("xt", "xin", T.xt[:, i, :, :], T.xin[:, :, 4 * i:4 * i + 4], more=True)
@@ -201,38 +174,74 @@ def rank_program(g, core, T, topo):
     quant("uq", "ut", T.uq[:], T.us[:], T.ut[:])
     quant("xq", "xt xqz", T.xq[:, 0:320], T.xs[:, 0:320], T.xt[:])
 
+    def constants0():
+        ts("iw2", "iw", T.iw[:], T.iw[:], 63, Op.bitwise_and)
+        fill("wm01", T.wm01[up], 0.0)
+        fill("pay0", T.pay[:, 40:41], 0.0)
+        ts("wm01", "iw2", T.wm01[lo], T.iw[lo], 0, Op.is_equal, more=True)
+        ts("cti2", "cti", T.cti[:], T.cti[:], 63, Op.bitwise_and)
+        ts("pj", "pi", T.pi[:, 4:6], T.pi[:, 0:2], 7, Op.bitwise_and)
+        fill("code0", T.cde[:], 1)
+
+    def constants3():
+        for c, w in ((0, 64), (64, 64), (128, 32)):
+            act("wat", "wm01", T.wat[:, c:c + w, :], T.wm01[:, 0:w, :], 0.625, more=c > 0)
+            act("wbt", "wm01", T.wbt[:, c:c + w, :], T.wm01[:, 0:w, :], -0.125, more=c > 0)
+        for j in range(3):
+            act("w3z", "zz", T.w3[:, j, :, :], T.zz[:], more=j > 0)
+        for j in range(2):
+            act("dg0", "zz", T.dg[:, 512 * j:512 * j + 512], T.zz[:], more=j > 0)
+        act("row0", "zz", T.row[:], T.zz[:, 0:400])
+
     def constants1():
-        quant("wa", "wat", T.waq[:], T.was[:], T.wat[:])
-        quant("wb", "wbt", T.wbq[:], T.wbs[:], T.wbt[:])
         ts("ct", "cti2", T.ct[:], T.cti[:], -1.0 / 512, Op.mult, 64.0625, Op.add)
         ts("s0", "pj", T.s0[:], T.pi[:, 4:6], 5.0, Op.mult, 64.0, Op.add)
+        ts("n40b", "n40", T.n40[:], T.n40[:], 63, Op.bitwise_and)
+        ts("ngm", "n40b", T.ngm[:], T.n40[:, 0:4], -1.0 / 512, Op.mult, 102560.0 / 512, Op.add)
+        ts("val0", "v0i", T.val0[:], T.val0[:], 64.4375, Op.add)
+        fill("tb0", T.tb[:, 50:51], 0.0)
+        fill("abk", T.ab[:, 0:150:3], 1 / EPS)
+        fill("dt0", T.dt3[:], 0.0)
 
     def constants2():
         for b in range(4):
             quant("e%d" % b, "et", T.eqc[:, 128 * b:128 * b + 128], T.eqs[:, 128 * b:128 * b + 128], T.et[:, 3 - b:515 - b])
             yield
-        for k, a in (("pt0", T.pt), ("dg0", T.dg), ("row0", T.row)):
-            fill(k, a[:], 0.0)
-            yield
         ts("pj2", "pi", T.pi[:, 6:8], T.pi[:, 0:2], 4, Op.logical_shift_right, 1, Op.bitwise_and)
         yield
-        ts("nb40", "n40", T.nb40[:], T.n40[:], 63, Op.bitwise_and, 4, Op.logical_shift_right)
-        yield
-        ts("n40b", "n40", T.n40[:], T.n40[:], 63, Op.bitwise_and)
+        ts("nb40", "n40b", T.nb40[:], T.n40[:], 4, Op.logical_shift_right)
         yield
         ts("nr2", "nr", T.nr[:], T.nr[:], 63, Op.bitwise_and)
-        yield
         yield
         ts("jr2", "jr", T.jr[:], T.jr[:], 15, Op.bitwise_and)
         yield
         copy("ngf", "n40b", T.ngf[:], T.n40[:, 0:4])
         yield
-        ts("ngm", "n40b", T.ngm[:], T.n40[:, 0:4], -1.0, Op.mult, 102560.0, Op.add)
+        fill("cqc1", T.cqc[:], -160.0)
+        yield
+        fill("one5", T.one5[:], 1.0)
+        yield
+        fill("pc0", T.pc[:], 0.0)
+        yield
+        fill("pk0", T.pk[:, 64:65], 0.0)
+        yield
+        fill("cqc1", T.cqc[:, 15:65:16], 0.0)
+        yield
+        fill("cf4", T.cf4[:, 0:4], 1024.0)
+        yield
+        fill("cf4", T.cf4[:, 4:8], 0.0, more=True)
+        yield
+        fill("cqc1", T.cqc[:, 64:65], 0.0)
+        yield
+        for a in (40, 208):
+            quant("dgqz", "zz", T.dgq[:, a:a + 128], T.dgs[:, a:a + 128], T.zz[:], more=True)
+            yield
+        quant("ptqz", "zz", T.ptq[:, 64:192], T.pts[:, 64:192], T.zz[:])
         yield
         for h, sl in ((0, lo), (1, up)):
             do("v", "w3z", "wt0", lambda: V.memset(T.w3[sl, 0, 64 * h:64 * h + 64, 1], 1.0), more=True)
             yield
-            ts("wt0", "ik w3z", T.w3[sl, 0, 64 * h:64 * h + 64, 0], T.ik[sl, :], 0, Op.is_ge, -1.0, Op.mult, more=True)
+            ts("wt0", "ik w3z", T.w3[sl, 0, 64 * h:64 * h + 64, 0], T.ik[sl, :], 0, Op.is_lt, more=True)
             yield
             for t in range(4):
                 ts("wt1", "nr2 ngf w3z", T.w3[sl, 1, 64 * h:64 * h + 64, t], T.nr[sl, :, t], T.ngf[sl, t:t + 1], Op.is_le, more=True)
@@ -273,6 +282,8 @@ def rank_program(g, core, T, topo):
         final = t == 2
         for i in range(5):
             mm("ps%d" % i, "xq uq", (ps[i][:, 0:128], T.xq[:, 64 * i:64 * i + 128], T.xs[:, 64 * i:64 * i + 128], T.uq[:], T.us[:]))
+        if t == 0:
+            constants0()
         for i in range(5):
             if i % 2:
                 act("sc", "ps%d" % i, T.sc[:, :, i], ps[i][:, 0:32], more=i > 0)
@@ -284,7 +295,9 @@ def rank_program(g, core, T, topo):
                 act("tp", "ps%d" % k, T.tp[:, 320 * b:320 * b + 320], ps[k][:, 0:320], 0.5, more=b > 0)
             act("tw", "tp", T.tw[:], T.tp[:])
 
-        if t > 0:
+        if t == 0:
+            constants3()
+        else:
             unpack()
         key = lambda a, b: T.sc[:, 3:32:4, a:b]
         for s in range(1, 5):
@@ -299,14 +312,17 @@ def rank_program(g, core, T, topo):
         tt("pay", "pac pad", T.pay[:, 0:40], T.pac[:], T.pad[:], Op.add)
         for r in range(3):
             ts("ne1%d" % r, "rk", T.ne1[:, r, :], T.rk[:], 4.0 - r, Op.not_equal)
-        if t == 0:
-            constants1()
         tt("d1a", "pay pay0", T.d1[:], T.pay[:, 0:40], T.pay[:, 1:41], Op.subtract)
         for r in range(3, 5):
             ts("ne1%d" % r, "rk", T.ne1[:, r, :], T.rk[:], 4.0 - r, Op.not_equal)
+        if t == 0:
+            quant("rqz", "zz", T.rq[:, 40:168], T.rs[:, 40:168], T.zz[:])
         copy("d1", "pay d1a", T.d1[:, 4:40:5], T.pay[:, 4:40:5])
         for r in range(5):
             scan("prb", "ne1%d d1" % r, T.prb[:, :, r], T.ne1[:, r, :], T.d1[:], more=True)
+        if t == 0:
+            quant("wa", "wat", T.waq[:], T.was[:], T.wat[:])
+            quant("wb", "wbt", T.wbq[:], T.wbs[:], T.wbt[:])
         for e in range(4):
             ts("rth%d" % e, "prb rt", T.rt[:, e:8:4, :, e], T.prb[:, 4 + 5 * e:40:20, :], M1 * 8, Op.add, M1 * 8, Op.subtract)
         for e in range(4):
@@ -316,87 +332,130 @@ def rank_program(g, core, T, topo):
             mm("ps%d" % k, "wa wb rq rqz",
                (ps[k][:, 0:128], T.waq[:, w:w + 128], T.was[:, w:w + 128], T.rq[:, 0:128], T.rs[:, 0:128]),
                (ps[k][:, 0:128], T.wbq[:, w:w + 128], T.wbs[:, w:w + 128], T.rq[:, 40:168], T.rs[:, 40:168]))
+        fill("abb", T.ab[:, 2:150:3], EPS)
+        if t == 0:
+            constants1()
         tt("tb1", "ps1 ct", T.tb[:, 10:30], ps[1][:, 0:20], T.ct[:, 10:30], Op.add)
         tt("tb2", "ps2 ct", T.tb[:, 30:50], ps[2][:, 20:40], T.ct[:, 30:50], Op.add)
         tt("tb3", "ps2 ct", T.tb[:, 0:10], ps[2][:, 30:40], T.ct[:, 0:10], Op.add)
         ts("aba", "val0 s0 abk", T.ab[:, 1:150:3], T.val0[:], T.s0[:, 0:1], Op.is_lt, EPS, Op.add)
-        fill("abb", T.ab[:, 2:150:3], EPS)
         tt("dtb", "tb1 tb2 tb3 tb0 dt0", T.dt3[:, 2:150:3], T.tb[:, 0:50], T.tb[:, 1:51], Op.subtract)
         tt("tbm", "val0 tb1 tb2 tb3", T.tbb[:], T.val0[:], T.tb[:, 0:50], Op.is_ge)
         scan("so0", "aba abb dtb", T.so[:, 0, :], T.ab[:], T.dt3[:])
         tt("tbb", "tbm", T.tbb[:], T.tbb[:], T.tb[:, 0:50], Op.mult)
+        def cd(n):
+            ts("cd%d" % n, "so%d ngm code0" % n, T.cde[:, n + 1:64:16], T.ngm[:], T.so[:, n, 149:150], Op.subtract, 512.0, Op.mult)
+
+        def ca(n):
+            ts("ca%d" % n, "cd%d" % n, T.ca[:, n + 1:64:16], T.cde[:, n + 1:64:16], 63, Op.bitwise_and)
+
+        def po(n):
+            ts("po%d" % n, "ca%d pt0" % n, T.pt[:, 4 * n + 4:256:64], T.ca[:, n + 1:64:16], 0, Op.is_equal)
+
+        def pe(n):
+            tt("pe%d" % n, "po%d pe%d pt0" % (n - 1, n - 1), T.pt[:, 4 * n + 5:256:64], T.pt[:, 4 * n + 1:256:64], T.pt[:, 4 * n:256:64], Op.add)
+
         for n in range(1, 14):
             s, so = T.so[:, n - 1, 149:150], "so%d" % (n - 1)
-            vk, vv = ("val0", T.val0) if n == 1 else ("val", T.val)
-            ts("aba", vk + " " + so, T.ab[:, 1:150:3], vv[:], s, Op.is_lt, EPS, Op.add)
-            ts("abb", "tbb " + so, T.ab[:, 2:150:3], T.tbb[:], s, Op.is_equal, EPS, Op.add)
+            vk, vv = ("val0", T.val0[:]) if n == 1 else ("vl%d" % ((n - 1) % 2), T.val[:, (n - 1) % 2, :])
             if n < 13:
                 ts("eq", so, T.eq[:], T.tb[:, 0:50], s, Op.is_equal, 64.0, Op.mult)
-            fillers(2)
-            scan("so%d" % n, "aba abb dtb", T.so[:, n, :], T.ab[:], T.dt3[:])
+            ts("aba", vk + " " + so, T.ab[:, 1:150:3], vv, s, Op.is_lt, EPS, Op.add)
+            ts("abb", "tbb " + so, T.ab[:, 2:150:3], T.tbb[:], s, Op.is_equal, EPS, Op.add)
+            cd(n - 1)
             if n < 13:
-                tt("val", vk + " eq", T.val[:], vv[:], T.eq[:], Op.subtract)
-            fillers(2)
+                tt("vl%d" % (n % 2), vk + " eq", T.val[:, n % 2, :], vv, T.eq[:], Op.subtract)
+            else:
+                fillers(2)
+            scan("so%d" % n, "aba abb dtb", T.so[:, n, :], T.ab[:], T.dt3[:])
+            if n >= 2:
+                po(n - 2)
+            if n >= 3:
+                pe(n - 2)
+            ca(n - 1)
+            fillers(4)
             if t == 0 and n == 5:
                 unpack()
         fillers(99)
-        y = T.so[:, :, 149]
-        for e in range(4):
-            ts("code%d" % e, "so0 so13 ngm code0", T.cde[:, 16 * e + 1:16 * e + 15], y, -512.0, Op.mult, T.ngm[:, e:e + 1], Op.add)
-        ts("phii", "so13", T.phii[:], y, -512.0, Op.mult, 102560.0, Op.add)
-        codes = "code0 code1 code2 code3"
-        ts("ca", codes, T.ca[:], T.cde[:], 63, Op.bitwise_and)
-        ts("cdf", codes, T.cdf[:], T.cde[:], 511, Op.bitwise_and)
+        cd(13)
+        ts("phii", "so0 so13", T.phii[:], T.so[:, :, 149], -512.0, Op.mult, 102560.0, Op.add)
+        po(12)
+        pe(12)
+        ca(13)
         ts("phij", "phii", T.phii[:], T.phii[:], 511, Op.bitwise_and)
-        ts("pto", "ca pt0", T.pt[:, 0:256:4], T.ca[:], 0, Op.is_equal)
+        pe(13)
+        po(13)
+        ts("cdf", " ".join("cd%d" % n for n in range(14)), T.cdf[:], T.cde[:], 511, Op.bitwise_and)
         ts("phi", "phij", T.phi[:], T.phii[:], -160.0, Op.add)
         for e in range(4):
             act("pc", "phi pc0", T.pc[:, 16 * e + 2:16 * e + 15], T.phi[:, 0:13], more=e > 0)
         act("pc", "phi cf4", T.pc[:, 0:64:16], T.cf4[:, 0:4], bias=T.phi[:, 13:14], more=True)
         act("pc", "phi cf4", T.pc[:, 1:64:16], T.cf4[:, 4:8], bias=T.phi[:, 13:14], more=True)
-        for i in range(2):
-            ts("nea", "cdf", T.nei[:, i, :], T.cdf[:], 64.0 * i, Op.not_equal, more=True)
-        scan("pti", "mk pto", T.pt[:, 1:256:4], T.mk[:], T.pt[:, 0:256:4])
-        for i in range(2, 4):
-            ts("nea", "cdf", T.nei[:, i, :], T.cdf[:], 64.0 * i, Op.not_equal, more=True)
-        copy("ptu", "pti", T.pt[:, 256:452:65], T.pt[:, 57:256:64])
-        ts("nea", "cdf", T.nei[:, 4, :], T.cdf[:], 256.0, Op.not_equal, more=True)
-        quant("ptq", "pto pti ptu ptqz", T.ptq[:, 0:128], T.pts[:, 0:128], T.pt[:])
+        tt("ptu", "pe13 po13 pt0", T.pt[:, 256:452:65], T.pt[:, 57:256:64], T.pt[:, 56:256:64], Op.add)
+        for i in range(3):
+            ts("nea", "cdf", T.nei[:, i, :], T.cdf[:], 64.0 * i, Op.not_equal, more=i > 0)
+        quant("ptq", "ptu ptqz " + " ".join("po%d" % n for n in range(14)) + " " + " ".join("pe%d" % n for n in range(1, 14)), T.ptq[:, 0:128], T.pts[:, 0:128], T.pt[:])
         mm("ps3", "ptq ptqz qwt0 qwt1", (ps[3][:, 0:128], *W3(0), T.ptq[:, 0:128], T.pts[:, 0:128]),
            (ps[3][:, 0:128], *W3(1), T.ptq[:, 64:192], T.pts[:, 64:192]))
+        for i in range(3, 5):
+            ts("nea", "cdf", T.nei[:, i, :], T.cdf[:], 64.0 * i, Op.not_equal, more=True)
         do("v", "nea", "nei", lambda: V.memset(T.nei[:, :, 0:64:16], 0.0))
         tt("dp", "pc pc0", T.dp[:], T.pc[:, 0:64], T.pc[:, 1:65], Op.subtract)
         for i in range(5):
             scan("uop", "nei dp", T.uop[:, i, :], T.nei[:, i, :], T.dp[:], more=True)
         up5 = T.uop[:, :, 14:64:16]
-        ts("fl", "uop", T.fl[:], up5, 512.0, Op.is_ge)
-        ts("flm", "uop", T.flm[:], up5, 512.0, Op.is_ge, -1024.0, Op.mult)
-        for e in range(4):
-            scan("inc", "fl one5", T.inc[:, e:20:4], T.one5[:, 0:5], T.fl[:, e:20:4], more=True, initial=-1.0)
-        tt("v2p", "uop flm", T.v2[:, 0:20], up5, T.flm[:], Op.add)
-        tt("pr", "fl inc", T.pr[:], T.fl[:], T.inc[:], Op.mult)
-        tt("pk", "ps3 cqc", T.pk[:, 0:64], ps[3][:, 0:64], T.cqc[:, 0:64], Op.add)
-        tt("dp", "pk pk0", T.dp[:], T.pk[:, 0:64], T.pk[:, 1:65], Op.subtract)
-        for i in range(5):
-            scan("uop", "nei dp", T.uop[:, i, :], T.nei[:, i, :], T.dp[:], more=i > 0)
-        tt("v2q", "uop pr", T.v2[:, 20:40], up5, T.pr[:], Op.add)
-        for nb in range(4):
-            tt("vm", "v2p v2q msk", T.vm[:, :, :, nb, :], T.v2[:], T.msk[:, nb, :], Op.mult, more=True)
-        ts("dgh", "vm dg0", T.dg[:, 160:320], T.vm[:], M1 * 32, Op.add, M1 * 32, Op.subtract)
-        tt("dgl", "vm dgh", T.dg[:, 0:160], T.vm[:], T.dg[:, 160:320], Op.subtract)
-        quant("dgq", "dgh dgl dgqz", T.dgq[:, 0:128], T.dgs[:, 0:128], T.dg[:])
-        mm("ps4", "dgq dgqz qwt2", (ps[4][:, 0:128], *W3(2), T.dgq[:, 0:128], T.dgs[:, 0:128]),
-           (ps[4][:, 0:128], *W3(2), T.dgq[:, 40:168], T.dgs[:, 40:168]))
-        ci = 1 if final else 0
-        ts("ofq", "ps4 cqo", T.ofq[:], ps[4][:, 20:40], T.cqo[:, ci:ci + 1], Op.add)
-        ts("ofp", "ps4", T.ofp[:], ps[4][:, 0:20], 160.0, Op.add)
-        do("v", "ofq phr row0", "row", lambda: V.tensor_copy(T.row[:].indirect(T.ofq[:, 0:20]), T.phr[:]))
-        for b in range(4):
+
+        def spread(x):
+            j = int(x == "q")
+            for nb in range(4):
+                tt("vm" + x, "v2%s msk" % x, T.vm[:, j, :, nb, :], T.v2[:, 20 * j:20 * j + 20], T.msk[:, nb, 0:20], Op.mult, more=nb > 0)
+
+        def digit(x, j):
+            c, m = 512 * int(x == "q"), T.vm[:, int(x == "q"), :, :, :]
+            if j:
+                ts("dh" + x, "vm%s dg0" % x, T.dg[:, c + 80:c + 160], m, M1 * 32, Op.add, M1 * 32, Op.subtract)
+            else:
+                tt("dl" + x, "vm%s dh%s" % (x, x), T.dg[:, c:c + 80], m, T.dg[:, c + 80:c + 160], Op.subtract)
+
+        def form(x, k):
+            c = 168 * (x == "q")
+            quant("dg" + x, "dh%s dl%s dgqz" % (x, x), T.dgq[:, c:c + 128], T.dgs[:, c:c + 128], T.dg[:, 512 * (x == "q"):512 * (x == "q") + 512])
+            mm("ps%d" % k, "dg%s dgqz qwt2" % x, (ps[k][:, 0:128], *W3(2), T.dgq[:, c:c + 128], T.dgs[:, c:c + 128]),
+               (ps[k][:, 0:128], *W3(2), T.dgq[:, c + 20:c + 148], T.dgs[:, c + 20:c + 148]))
+
+        def blend(b):
             cs = slice(320 * b, 320 * b + 320)
             tt("zp%d" % b, "tp tw ofp", T.zp[:, cs], T.tw[:, cs].indirect(T.ofp[:, 0:20]), T.tp[:, cs], Op.add)
+
+        tt("pk", "ps3 cqc", T.pk[:, 0:64], ps[3][:, 0:64], T.cqc[:, 0:64], Op.add)
+        ts("fl", "uop", T.fl[:], up5, 512.0, Op.is_ge)
+        ts("flm", "uop", T.flm[:], up5, 512.0, Op.is_ge, -1024.0, Op.mult)
+        tt("dp", "pk pk0", T.dp[:], T.pk[:, 0:64], T.pk[:, 1:65], Op.subtract)
+        tt("v2p", "uop flm", T.v2[:, 0:20], up5, T.flm[:], Op.add)
+        for e in range(4):
+            scan("inc", "fl one5", T.inc[:, e:20:4], T.one5[:, 0:5], T.fl[:, e:20:4], more=True, initial=-1.0)
+        for i in range(5):
+            scan("uop", "nei dp", T.uop[:, i, :], T.nei[:, i, :], T.dp[:], more=i > 0)
+        tt("pr", "fl inc", T.pr[:], T.fl[:], T.inc[:], Op.mult)
+        spread("p")
+        tt("v2q", "uop pr", T.v2[:, 20:40], up5, T.pr[:], Op.add)
+        digit("p", 1)
+        spread("q")
+        digit("p", 0)
+        digit("q", 1)
+        form("p", 5)
+        digit("q", 0)
+        form("q", 4)
+        ts("ofp", "ps5", T.ofp[:], ps[5][:, 0:20], 160.0, Op.add)
+        blend(0)
+        ci = 1 if final else 0
+        ts("ofq", "ps4 cqo", T.ofq[:], ps[4][:, 0:20], T.cqo[:, ci:ci + 1], Op.add)
+        do("v", "ofq phr row0", "row", lambda: V.tensor_copy(T.row[:].indirect(T.ofq[:, 0:20]), T.phr[:]))
+        blend(1)
         if final:
             for a in range(2):
                 do("v", "row", "tr", lambda: V.transpose(T.trl[:, a, :], T.row[:, 16 * a:16 * a + 320]), more=a > 0)
+            blend(2)
             for a in range(2):
                 ts("te%d" % a, "tr me", T.te[:, a:20:2], T.trl[:, a, 0:320:32], T.me[:, 0:1], Op.mult)
                 ts("to%d" % a, "tr mo", T.to[:, a:20:2], T.trl[:, a, 16:320:32], T.mo[:, 0:1], Op.mult)
@@ -405,10 +464,12 @@ def rank_program(g, core, T, topo):
                 for a in range(2):
                     c = i + 80 * a
                     do("v", "row", "tr", lambda: V.transpose(T.tr[:, i, a, :], T.row[:, c:c + 316:5]), more=i + a > 0)
+            blend(2)
             for h in range(2):
                 sl = slice(10 * h, 10 * h + 10)
                 ts("te%d" % h, "tr me", T.te[:, sl], T.tr[:, :, :, 32 * h], T.me[:, 0:1], Op.mult)
                 ts("to%d" % h, "tr mo", T.to[:, sl], T.tr[:, :, :, 32 * h + 16], T.mo[:, 0:1], Op.mult)
+        blend(3)
         tt("ql", "te0 te1 to0 to1", T.to[:], T.te[:], T.to[:], Op.add)
         copy("off0", "ql", T.off[:], T.to[:])
 

import numpy as np
from concourse.mybir import dt, AluOpType as Op, ActivationFunctionType as AF

F, B, I, U16 = "float32", "bfloat16", "int32", "uint16"
C8, U8 = "float8_e4m3fn_x4", "uint8"


def _sb(t, *s):
    return ("sbuf", [128] + list(s), t)


SCRATCH = {
    "xin": _sb(B, 64, 20), "xt": _sb(B, 5, 64, 4), "xl": _sb(B, 1280), "ut": _sb(B, 512), "vt": _sb(B, 512),
    "xq": _sb(C8, 384), "xs": _sb(U8, 384), "uq": _sb(C8, 128), "us": _sb(U8, 128), "vq": _sb(C8, 128), "vs": _sb(U8, 128),
    "wq": _sb(C8, 512), "wsc": _sb(U8, 512), "lq": _sb(C8, 320), "lsc": _sb(U8, 320),
    "sc": _sb(F, 32, 5), "cm": _sb(F, 4, 8, 5), "a2": _sb(F, 2, 8, 5), "rk": _sb(F, 40), "pb": _sb(F, 3, 8, 5),
    "pac": _sb(F, 40), "pad": _sb(F, 40), "pay": _sb(F, 41), "d1": _sb(F, 40), "ne1": _sb(F, 5, 40), "prb": _sb(F, 40, 5),
    "rt": _sb(B, 26, 5, 4), "rq": _sb(C8, 168), "rs": _sb(U8, 168),
    "tb": _sb(F, 51), "tbb": _sb(F, 50), "val": _sb(F, 2, 50), "eq": _sb(F, 50), "ab": _sb(F, 150), "dt3": _sb(F, 150), "so": _sb(F, 14, 150),
    "phii": _sb(I, 14), "cdf": _sb(I, 64), "phi": _sb(F, 14), "cde": _sb(I, 64), "ca": _sb(I, 64), "pt": _sb(B, 512),
    "ptq": _sb(C8, 192), "pts": _sb(U8, 192), "nei": _sb(F, 5, 64), "pc": _sb(F, 65), "dp": _sb(F, 64), "uop": _sb(F, 5, 64),
    "fl": _sb(F, 20), "flm": _sb(F, 20), "inc": _sb(F, 20), "pr": _sb(F, 20), "pk": _sb(F, 65),
    "v2": _sb(F, 40), "vm": _sb(F, 2, 5, 4, 4), "dg": _sb(B, 1024), "dgq": _sb(C8, 336), "dgs": _sb(U8, 336),
    "ofp": _sb(U16, 20), "ofq": _sb(U16, 20), "row": _sb(F, 400),
    "tr": _sb(F, 5, 2, 64), "trl": _sb(F, 2, 320), "te": _sb(F, 20), "to": _sb(F, 20), "off": _sb(U16, 20),
    "tp": _sb(B, 1280), "tw": _sb(B, 1280), "zp": _sb(B, 1280), "zt": _sb(B, 1280), "at": _sb(B, 1280), "tm": _sb(F, 8, 160), "yb": _sb(F, 320),
    "zz": _sb(B, 512), "iw": _sb(I, 64, 4), "wm01": _sb(B, 64, 4), "wat": _sb(B, 160, 4), "wbt": _sb(B, 160, 4),
    "waq": _sb(C8, 160), "was": _sb(U8, 160), "wbq": _sb(C8, 160), "wbs": _sb(U8, 160),
    "et": _sb(B, 516), "ones": _sb(B, 128), "eqc": _sb(C8, 512), "eqs": _sb(U8, 512),
    "w3": _sb(B, 3, 128, 4),
    "cq3": _sb(C8, 384), "cs3": _sb(U8, 384),
    "ik": _sb(I, 64), "nr": _sb(I, 64, 4), "jr": _sb(I, 16, 4),
    "n40": _sb(I, 40), "nb40": _sb(I, 40), "msk": _sb(F, 4, 40), "ngf": _sb(F, 4), "ngm": _sb(F, 4),
    "cti": _sb(I, 50), "ct": _sb(F, 50), "val0": _sb(F, 50),
    "pi": _sb(I, 8), "s0": _sb(F, 2), "me": _sb(F, 2), "mo": _sb(F, 2), "cqo": _sb(F, 2),
    "ci2": _sb(F, 40), "cqc": _sb(F, 65), "one5": _sb(F, 8), "cf4": _sb(F, 8), "phr": _sb(F, 320), "lgr": _sb(F, 320),
}
for _k in ("send", "stay", "land"):
    SCRATCH[_k + "c"] = _sb(C8, 480)
    SCRATCH[_k + "p"] = _sb(U8, 480)
for _t in range(8):
    SCRATCH["ps%d" % _t] = ("psum", [128, 512], F)
SEMAPHORES = ["v", "s", "t", "p", "dx", "du", "dw", "dv", "fin"] + ["%s%d" % (a, i) for a in ("arr", "snd") for i in range(3)]

M1 = 12582912.0
EPS = 2.0 ** -30
PARTNER = [1, 2, 3]


def rank_program(g, core, T, topo):
    rank = T.rank_of(core)
    if rank is None:
        return
    queue = {"v": g.vector, "s": g.scalar, "t": g.tensor, "p": g, "y": g.sync}
    count, known, last, reads = {}, {e: {} for e in queue}, {}, {}

    def need(e, sem, val):
        if known[e].get(sem, 0) < val:
            queue[e].wait_ge(T.sem[sem], val)
            known[e][sem] = val

    def pre(e, rd, wr):
        for k in rd.split():
            for s, n in last.get(k, {}).items():
                need(e, s, n)
        for k in wr.split():
            for s, n in list(last.get(k, {}).items()) + list(reads.get(k, {}).items()):
                need(e, s, n)

    def post(sem, n, rd, wr, more=False):
        count[sem] = count.get(sem, 0) + n
        for k in rd.split():
            reads.setdefault(k, {})[sem] = count[sem]
        for k in wr.split():
            old = last.get(k, {}) if more else {}
            last[k] = {**old, sem: count[sem]}
            if not more:
                reads[k] = {}

    def do(e, rd, wr, call, sem=None, n=1, more=False):
        pre(e, rd, "" if more else wr)
        if e == "p":
            need("p", "p", count.get("p", 0))
        if more:
            for k in wr.split():
                for s, c in reads.get(k, {}).items():
                    if s != e:
                        need(e, s, c)
        sem = sem or e
        call().then_inc(T.sem[sem], n)
        post(sem, n, rd, wr, more)

    V, S, P, Y = g.vector, g.scalar, g, g.sync

    def tt(wr, rd, out, a, b, op, more=False):
        do("v", rd, wr, lambda: V.tensor_tensor(out, a, b, op), more=more)

    def ts(wr, rd, out, a, s1, op0, s2=None, op1=None, more=False):
        if op1 is None:
            do("v", rd, wr, lambda: V.tensor_scalar(out, a, s1, None, op0), more=more)
        else:
            do("v", rd, wr, lambda: V.tensor_scalar(out, a, s1, s2, op0, op1), more=more)

    def scan(wr, rd, out, a, b, more=False, initial=0.0):
        do("v", rd, wr, lambda: V.tensor_tensor_scan(out, a, b, initial, Op.mult, Op.add), more=more)

    def copy(wr, rd, out, a, more=False):
        do("v", rd, wr, lambda: V.tensor_copy(out, a), more=more)

    def fill(wr, out, c, more=False):
        do("v", "", wr, lambda: V.memset(out, c), more=more)

    def quant(wr, rd, q, s, t, more=False):
        do("v", rd, wr, lambda: V.quantize_mx(q, s, t), more=more)

    def act(wr, rd, out, a, scale=None, more=False, bias=None):
        if bias is not None:
            do("s", rd, wr, lambda: S.activation(out, a, AF.Identity, bias=bias), more=more)
        elif scale is None:
            do("s", rd, wr, lambda: S.activation(out, a, AF.Copy), more=more)
        else:
            do("s", rd, wr, lambda: S.activation(out, a, AF.Copy, scale=scale), more=more)

    def iota(wr, out, pat, base, cm, more=False):
        do("p", "", wr, lambda: P.iota(out, pat, base, cm), more=more)

    def iotaf(wr, out, pat, base, cm):
        do("p", "", wr, lambda: P.iota(out, pat, base, cm, allow_small_or_imprecise_dtypes=True))

    def mm(wr, rd, *prods):
        pre("t", rd, wr)
        for i, p in enumerate(prods):
            ins = g.tensor.matmul_mx(*p, i == 0, i == len(prods) - 1)
        ins.then_inc(T.sem.t, 1)
        post("t", 1, rd, wr)

    do("y", "", "xin", lambda: Y.dma_start(T.xin[:], T.x[:]), "dx", 16)
    for G in range(8):
        gg = 7 - G
        q = ("s", S) if G % 2 else ("y", Y)
        do(q[0], "", "ut", lambda: q[1].dma_start(T.ut[:, 16 * G:16 * G + 16], T.u[:, 64 * gg:64 * gg + 16]), "du", 16, more=True)
    do("s", "", "ut", lambda: S.dma_start(T.ut[:, 128:512], T.u[:, 128:512]), "du", 16, more=True)
    do("s", "", "wq", lambda: S.dma_start(T.wq[:].bitcast(dt.uint8), T.wc[:]), "dw", 16, more=True)
    do("s", "", "wq", lambda: S.dma_start(T.wsc[:], T.ws[:]), "dw", 16, more=True)
    do("y", "", "vt", lambda: Y.dma_start(T.vt[:], T.v[:]), "dv", 16)

    lo, up = slice(0, 64), slice(64, 128)
    iota("iw", T.iw[:], [[-1, 64], [8, 4]], -56, 1)
    iota("cti", T.cti[:], [[-8, 10], [0, 5]], 72, 1)
    iota("pi", T.pi[:, 0:4], [[0, 4]], 0, 1)
    fill("et0", T.et[:], 0.0)
    fill("ones", T.ones[:], 1.0)
    do("p", "ones et0", "et", lambda: P.affine_select(T.et[:, 3:515:4], T.ones[:], [[-1, 128]], Op.is_equal, 0.0, 0, 1))
    iotaf("v0i", T.val0[:], [[-1, 50]], 49, 0)
    iotaf("ci2", T.ci2[:], [[0, 8], [1, 5]], -2, 0)
    for h, sl in ((0, lo), (1, up)):
        iota("n40", T.n40[sl, :], [[0, 10], [8, 4]], 32 * h, 1, more=True)
        iota("nr", T.nr[sl, :, :], [[1, 64], [8, 4]], 32 * h, 0, more=True)
        iota("ik", T.ik[sl, :], [[-1, 64]], 0, 1, more=True)
    iota("jr", T.jr[:], [[1, 16], [-8, 4]], 0, -1)
    iotaf("phr", T.phr[:], [[1, 320]], 0, 0)
    iotaf("lgr", T.lgr[:], [[1, 5], [5, 64]], 0, 0)

    fill("zz", T.zz[:], 0.0)
    quant("xqz", "zz", T.xq[:, 256:384], T.xs[:, 256:384], T.zz[:])
    act("rt", "zz", T.rt[:, 0:25, :, :], T.zz[:, 0:500])
    act("rt", "zz", T.rt[:, 25, :, :], T.zz[:, 0:20], more=True)
    act("pt0", "zz", T.pt[:], T.zz[:])
    for i in range(5):
        if i < 3:
            copy("xt", "xin", T.xt[:, i, :, :], T.xin[:, :, 4 * i:4 * i + 4], more=True)
        else:
            act("xt", "xin", T.xt[:, i, :, :], T.xin[:, :, 4 * i:4 * i + 4], more=True)
    quant("uq", "ut", T.uq[:], T.us[:], T.ut[:])
    quant("xq", "xt xqz", T.xq[:, 0:320], T.xs[:, 0:320], T.xt[:])

    def constants0():
        ts("iw2", "iw", T.iw[:], T.iw[:], 63, Op.bitwise_and)
        fill("wm01", T.wm01[up], 0.0)
        fill("pay0", T.pay[:, 40:41], 0.0)
        ts("wm01", "iw2", T.wm01[lo], T.iw[lo], 0, Op.is_equal, more=True)
        ts("cti2", "cti", T.cti[:], T.cti[:], 63, Op.bitwise_and)
        ts("pj", "pi", T.pi[:, 4:6], T.pi[:, 0:2], 7, Op.bitwise_and)
        fill("code0", T.cde[:], 1)

    def constants3():
        for c, w in ((0, 64), (64, 64), (128, 32)):
            act("wat", "wm01", T.wat[:, c:c + w, :], T.wm01[:, 0:w, :], 0.625, more=c > 0)
            act("wbt", "wm01", T.wbt[:, c:c + w, :], T.wm01[:, 0:w, :], -0.125, more=c > 0)
        for j in range(3):
            act("w3z", "zz", T.w3[:, j, :, :], T.zz[:], more=j > 0)
        for j in range(2):
            act("dg0", "zz", T.dg[:, 512 * j:512 * j + 512], T.zz[:], more=j > 0)
        act("row0", "zz", T.row[:], T.zz[:, 0:400])

    def constants1():
        ts("ct", "cti2", T.ct[:], T.cti[:], -1.0 / 512, Op.mult, 64.0625, Op.add)
        ts("s0", "pj", T.s0[:], T.pi[:, 4:6], 5.0, Op.mult, 64.0, Op.add)
        ts("n40b", "n40", T.n40[:], T.n40[:], 63, Op.bitwise_and)
        ts("ngm", "n40b", T.ngm[:], T.n40[:, 0:4], -1.0 / 512, Op.mult, 102560.0 / 512, Op.add)
        ts("val0", "v0i", T.val0[:], T.val0[:], 64.4375, Op.add)
        fill("tb0", T.tb[:, 50:51], 0.0)
        fill("abk", T.ab[:, 0:150:3], 1 / EPS)
        fill("dt0", T.dt3[:], 0.0)

    def constants2():
        for b in range(4):
            quant("e%d" % b, "et", T.eqc[:, 128 * b:128 * b + 128], T.eqs[:, 128 * b:128 * b + 128], T.et[:, 3 - b:515 - b])
            yield
        ts("pj2", "pi", T.pi[:, 6:8], T.pi[:, 0:2], 4, Op.logical_shift_right, 1, Op.bitwise_and)
        yield
        ts("nb40", "n40b", T.nb40[:], T.n40[:], 4, Op.logical_shift_right)
        yield
        ts("nr2", "nr", T.nr[:], T.nr[:], 63, Op.bitwise_and)
        yield
        ts("jr2", "jr", T.jr[:], T.jr[:], 15, Op.bitwise_and)
        yield
        copy("ngf", "n40b", T.ngf[:], T.n40[:, 0:4])
        yield
        fill("cqc1", T.cqc[:], -160.0)
        yield
        fill("one5", T.one5[:], 1.0)
        yield
        fill("pc0", T.pc[:], 0.0)
        yield
        fill("pk0", T.pk[:, 64:65], 0.0)
        yield
        fill("cqc1", T.cqc[:, 15:65:16], 0.0)
        yield
        fill("cf4", T.cf4[:, 0:4], 1024.0)
        yield
        fill("cf4", T.cf4[:, 4:8], 0.0, more=True)
        yield
        fill("cqc1", T.cqc[:, 64:65], 0.0)
        yield
        for a in (40, 208):
            quant("dgqz", "zz", T.dgq[:, a:a + 128], T.dgs[:, a:a + 128], T.zz[:], more=True)
            yield
        quant("ptqz", "zz", T.ptq[:, 64:192], T.pts[:, 64:192], T.zz[:])
        yield
        for h, sl in ((0, lo), (1, up)):
            do("v", "w3z", "wt0", lambda: V.memset(T.w3[sl, 0, 64 * h:64 * h + 64, 1], 1.0), more=True)
            yield
            ts("wt0", "ik w3z", T.w3[sl, 0, 64 * h:64 * h + 64, 0], T.ik[sl, :], 0, Op.is_lt, more=True)
            yield
            for t in range(4):
                ts("wt1", "nr2 ngf w3z", T.w3[sl, 1, 64 * h:64 * h + 64, t], T.nr[sl, :, t], T.ngf[sl, t:t + 1], Op.is_le, more=True)
                yield
                m = 64 * h + 16 * t
                ts("wt2", "jr2 w3z", T.w3[sl, 2, m:m + 16, t], T.jr[sl, :, t], 0, Op.is_equal, more=True)
                yield
        ts("cqc", "n40b cqc1", T.cqc[:, 0:64:16], T.n40[:, 0:4], 5.0, Op.mult, -160.0, Op.add)
        yield
        for j in range(3):
            quant("qwt%d" % j, "wt%d" % j, T.cq3[:, 128 * j:128 * j + 128], T.cs3[:, 128 * j:128 * j + 128], T.w3[:, j, :, :])
            yield
            yield
        for nb in range(4):
            ts("msk", "nb40", T.msk[:, nb, :], T.nb40[:], nb, Op.is_equal, more=True)
            yield
        copy("mo", "pj2", T.mo[:], T.pi[:, 6:8])
        yield
        ts("me", "pj2", T.me[:], T.pi[:, 6:8], -1.0, Op.mult, 1.0, Op.add)
        yield
        ts("cqo", "pj2", T.cqo[:, 0:1], T.pi[:, 6:7], 80.0, Op.mult, 160.0, Op.add)
        yield
        ts("cqo", "pj2", T.cqo[:, 1:2], T.pi[:, 6:7], 16.0, Op.mult, 160.0, Op.add, more=True)

    rest = constants2()

    def fillers(n):
        for _ in range(n):
            next(rest, None)

    def W3(j):
        return T.cq3[:, 128 * j:128 * j + 128], T.cs3[:, 128 * j:128 * j + 128]

    ps = [T["ps%d" % i] for i in range(8)]
    partner_of = lambda t: T.cores[rank ^ PARTNER[t]]

    for t in range(3):
        final = t == 2
        for i in range(5):
            mm("ps%d" % i, "xq uq", (ps[i][:, 0:128], T.xq[:, 64 * i:64 * i + 128], T.xs[:, 64 * i:64 * i + 128], T.uq[:], T.us[:]))
        if t == 0:
            constants0()
        for i in range(5):
            if i % 2:
                act("sc", "ps%d" % i, T.sc[:, :, i], ps[i][:, 0:32], more=i > 0)
            else:
                copy("sc", "ps%d" % i, T.sc[:, :, i], ps[i][:, 0:32], more=i > 0)
        def unpack():
            for b, k in enumerate((5, 6, 7, 0)):
                mm("ps%d" % k, "xq e%d" % b, (ps[k][:, 0:320], T.eqc[:, 128 * b:128 * b + 128], T.eqs[:, 128 * b:128 * b + 128], T.xq[:, 0:320], T.xs[:, 0:320]))
                act("tp", "ps%d" % k, T.tp[:, 320 * b:320 * b + 320], ps[k][:, 0:320], 0.5, more=b > 0)
            act("tw", "tp", T.tw[:], T.tp[:])

        if t == 0:
            constants3()
        else:
            unpack()
        key = lambda a, b: T.sc[:, 3:32:4, a:b]
        for s in range(1, 5):
            tt("cm", "sc", T.cm[:, s - 1, :, 0:5 - s], key(s, 5), key(0, 5 - s), Op.is_gt, more=True)
            tt("cm", "sc", T.cm[:, s - 1, :, 5 - s:5], key(0, s), key(5 - s, 5), Op.is_ge, more=True)
        for b in range(3):
            ts("pb%d" % b, "sc", T.pb[:, b, :, :], T.sc[:, b:32:4, :], 0.0, Op.is_gt, 32.0 / 2 ** b, Op.mult)
        tt("a2", "cm", T.a2[:], T.cm[:, 0:2, :, :], T.cm[:, 2:4, :, :], Op.add)
        tt("pac", "pb0 pb1", T.pac[:], T.pb[:, 0, :, :], T.pb[:, 1, :, :], Op.add)
        tt("pad", "pb2 ci2", T.pad[:], T.pb[:, 2, :, :], T.ci2[:], Op.add)
        tt("rk", "a2", T.rk[:], T.a2[:, 0, :, :], T.a2[:, 1, :, :], Op.add)
        tt("pay", "pac pad", T.pay[:, 0:40], T.pac[:], T.pad[:], Op.add)
        for r in range(3):
            ts("ne1%d" % r, "rk", T.ne1[:, r, :], T.rk[:], 4.0 - r, Op.not_equal)
        tt("d1a", "pay pay0", T.d1[:], T.pay[:, 0:40], T.pay[:, 1:41], Op.subtract)
        for r in range(3, 5):
            ts("ne1%d" % r, "rk", T.ne1[:, r, :], T.rk[:], 4.0 - r, Op.not_equal)
        if t == 0:
            quant("rqz", "zz", T.rq[:, 40:168], T.rs[:, 40:168], T.zz[:])
        copy("d1", "pay d1a", T.d1[:, 4:40:5], T.pay[:, 4:40:5])
        for r in range(5):
            scan("prb", "ne1%d d1" % r, T.prb[:, :, r], T.ne1[:, r, :], T.d1[:], more=True)
        if t == 0:
            quant("wa", "wat", T.waq[:], T.was[:], T.wat[:])
            quant("wb", "wbt", T.wbq[:], T.wbs[:], T.wbt[:])
        for e in range(4):
            ts("rth%d" % e, "prb rt", T.rt[:, e:8:4, :, e], T.prb[:, 4 + 5 * e:40:20, :], M1 * 8, Op.add, M1 * 8, Op.subtract)
        for e in range(4):
            tt("rtl%d" % e, "prb rth%d" % e, T.rt[:, 8 + e:16:4, :, e], T.prb[:, 4 + 5 * e:40:20, :], T.rt[:, e:8:4, :, e], Op.subtract)
        quant("rq", "rqz rth0 rth1 rth2 rth3 rtl0 rtl1 rtl2 rtl3", T.rq[:, 0:130], T.rs[:, 0:130], T.rt[:])
        for k, w in ((1, 0), (2, 32)):
            mm("ps%d" % k, "wa wb rq rqz",
               (ps[k][:, 0:128], T.waq[:, w:w + 128], T.was[:, w:w + 128], T.rq[:, 0:128], T.rs[:, 0:128]),
               (ps[k][:, 0:128], T.wbq[:, w:w + 128], T.wbs[:, w:w + 128], T.rq[:, 40:168], T.rs[:, 40:168]))
        fill("abb", T.ab[:, 2:150:3], EPS)
        if t == 0:
            constants1()
        tt("tb1", "ps1 ct", T.tb[:, 10:30], ps[1][:, 0:20], T.ct[:, 10:30], Op.add)
        tt("tb2", "ps2 ct", T.tb[:, 30:50], ps[2][:, 20:40], T.ct[:, 30:50], Op.add)
        tt("tb3", "ps2 ct", T.tb[:, 0:10], ps[2][:, 30:40], T.ct[:, 0:10], Op.add)
        ts("aba", "val0 s0 abk", T.ab[:, 1:150:3], T.val0[:], T.s0[:, 0:1], Op.is_lt, EPS, Op.add)
        tt("dtb", "tb1 tb2 tb3 tb0 dt0", T.dt3[:, 2:150:3], T.tb[:, 0:50], T.tb[:, 1:51], Op.subtract)
        tt("tbm", "val0 tb1 tb2 tb3", T.tbb[:], T.val0[:], T.tb[:, 0:50], Op.is_ge)
        scan("so0", "aba abb dtb", T.so[:, 0, :], T.ab[:], T.dt3[:])
        tt("tbb", "tbm", T.tbb[:], T.tbb[:], T.tb[:, 0:50], Op.mult)
        def cd(n):
            ts("cd%d" % n, "so%d ngm code0" % n, T.cde[:, n + 1:64:16], T.ngm[:], T.so[:, n, 149:150], Op.subtract, 512.0, Op.mult)

        def ca(n):
            ts("ca%d" % n, "cd%d" % n, T.ca[:, n + 1:64:16], T.cde[:, n + 1:64:16], 63, Op.bitwise_and)

        def po(n):
            ts("po%d" % n, "ca%d pt0" % n, T.pt[:, 4 * n + 4:256:64], T.ca[:, n + 1:64:16], 0, Op.is_equal)

        def pe(n):
            tt("pe%d" % n, "po%d pe%d pt0" % (n - 1, n - 1), T.pt[:, 4 * n + 5:256:64], T.pt[:, 4 * n + 1:256:64], T.pt[:, 4 * n:256:64], Op.add)

        for n in range(1, 14):
            s, so = T.so[:, n - 1, 149:150], "so%d" % (n - 1)
            vk, vv = ("val0", T.val0[:]) if n == 1 else ("vl%d" % ((n - 1) % 2), T.val[:, (n - 1) % 2, :])
            if n < 13:
                ts("eq", so, T.eq[:], T.tb[:, 0:50], s, Op.is_equal, 64.0, Op.mult)
            ts("aba", vk + " " + so, T.ab[:, 1:150:3], vv, s, Op.is_lt, EPS, Op.add)
            ts("abb", "tbb " + so, T.ab[:, 2:150:3], T.tbb[:], s, Op.is_equal, EPS, Op.add)
            cd(n - 1)
            if n < 13:
                tt("vl%d" % (n % 2), vk + " eq", T.val[:, n % 2, :], vv, T.eq[:], Op.subtract)
            else:
                fillers(2)
            scan("so%d" % n, "aba abb dtb", T.so[:, n, :], T.ab[:], T.dt3[:])
            if n >= 2:
                po(n - 2)
            if n >= 3:
                pe(n - 2)
            ca(n - 1)
            fillers(4)
            if t == 0 and n == 5:
                unpack()
        fillers(99)
        cd(13)
        ts("phii", "so0 so13", T.phii[:], T.so[:, :, 149], -512.0, Op.mult, 102560.0, Op.add)
        po(12)
        pe(12)
        ca(13)
        ts("phij", "phii", T.phii[:], T.phii[:], 511, Op.bitwise_and)
        pe(13)
        po(13)
        ts("cdf", " ".join("cd%d" % n for n in range(14)), T.cdf[:], T.cde[:], 511, Op.bitwise_and)
        ts("phi", "phij", T.phi[:], T.phii[:], -160.0, Op.add)
        for e in range(4):
            act("pc", "phi pc0", T.pc[:, 16 * e + 2:16 * e + 15], T.phi[:, 0:13], more=e > 0)
        act("pc", "phi cf4", T.pc[:, 0:64:16], T.cf4[:, 0:4], bias=T.phi[:, 13:14], more=True)
        act("pc", "phi cf4", T.pc[:, 1:64:16], T.cf4[:, 4:8], bias=T.phi[:, 13:14], more=True)
        tt("ptu", "pe13 po13 pt0", T.pt[:, 256:452:65], T.pt[:, 57:256:64], T.pt[:, 56:256:64], Op.add)
        for i in range(3):
            ts("nea", "cdf", T.nei[:, i, :], T.cdf[:], 64.0 * i, Op.not_equal, more=i > 0)
        quant("ptq", "ptu ptqz " + " ".join("po%d" % n for n in range(14)) + " " + " ".join("pe%d" % n for n in range(1, 14)), T.ptq[:, 0:128], T.pts[:, 0:128], T.pt[:])
        mm("ps3", "ptq ptqz qwt0 qwt1", (ps[3][:, 0:128], *W3(0), T.ptq[:, 0:128], T.pts[:, 0:128]),
           (ps[3][:, 0:128], *W3(1), T.ptq[:, 64:192], T.pts[:, 64:192]))
        for i in range(3, 5):
            ts("nea", "cdf", T.nei[:, i, :], T.cdf[:], 64.0 * i, Op.not_equal, more=True)
        do("v", "nea", "nei", lambda: V.memset(T.nei[:, :, 0:64:16], 0.0))
        tt("dp", "pc pc0", T.dp[:], T.pc[:, 0:64], T.pc[:, 1:65], Op.subtract)
        for i in range(5):
            scan("uop", "nei dp", T.uop[:, i, :], T.nei[:, i, :], T.dp[:], more=True)
        up5 = T.uop[:, :, 14:64:16]

        def spread(x):
            j = int(x == "q")
            for nb in range(4):
                tt("vm" + x, "v2%s msk" % x, T.vm[:, j, :, nb, :], T.v2[:, 20 * j:20 * j + 20], T.msk[:, nb, 0:20], Op.mult, more=nb > 0)

        def digit(x, j):
            c, m = 512 * int(x == "q"), T.vm[:, int(x == "q"), :, :, :]
            if j:
                ts("dh" + x, "vm%s dg0" % x, T.dg[:, c + 80:c + 160], m, M1 * 32, Op.add, M1 * 32, Op.subtract)
            else:
                tt("dl" + x, "vm%s dh%s" % (x, x), T.dg[:, c:c + 80], m, T.dg[:, c + 80:c + 160], Op.subtract)

        def form(x, k):
            c = 168 * (x == "q")
            quant("dg" + x, "dh%s dl%s dgqz" % (x, x), T.dgq[:, c:c + 128], T.dgs[:, c:c + 128], T.dg[:, 512 * (x == "q"):512 * (x == "q") + 512])
            mm("ps%d" % k, "dg%s dgqz qwt2" % x, (ps[k][:, 0:128], *W3(2), T.dgq[:, c:c + 128], T.dgs[:, c:c + 128]),
               (ps[k][:, 0:128], *W3(2), T.dgq[:, c + 20:c + 148], T.dgs[:, c + 20:c + 148]))

        def blend(b):
            cs = slice(320 * b, 320 * b + 320)
            tt("zp%d" % b, "tp tw ofp", T.zp[:, cs], T.tw[:, cs].indirect(T.ofp[:, 0:20]), T.tp[:, cs], Op.add)

        tt("pk", "ps3 cqc", T.pk[:, 0:64], ps[3][:, 0:64], T.cqc[:, 0:64], Op.add)
        ts("fl", "uop", T.fl[:], up5, 512.0, Op.is_ge)
        ts("flm", "uop", T.flm[:], up5, 512.0, Op.is_ge, -1024.0, Op.mult)
        tt("dp", "pk pk0", T.dp[:], T.pk[:, 0:64], T.pk[:, 1:65], Op.subtract)
        tt("v2p", "uop flm", T.v2[:, 0:20], up5, T.flm[:], Op.add)
        for e in range(4):
            scan("inc", "fl one5", T.inc[:, e:20:4], T.one5[:, 0:5], T.fl[:, e:20:4], more=True, initial=-1.0)
        for i in range(5):
            scan("uop", "nei dp", T.uop[:, i, :], T.nei[:, i, :], T.dp[:], more=i > 0)
        tt("pr", "fl inc", T.pr[:], T.fl[:], T.inc[:], Op.mult)
        spread("p")
        tt("v2q", "uop pr", T.v2[:, 20:40], up5, T.pr[:], Op.add)
        digit("p", 1)
        spread("q")
        digit("p", 0)
        digit("q", 1)
        form("p", 5)
        digit("q", 0)
        form("q", 4)
        ts("ofp", "ps5", T.ofp[:], ps[5][:, 0:20], 160.0, Op.add)
        blend(0)
        ci = 1 if final else 0
        ts("ofq", "ps4 cqo", T.ofq[:], ps[4][:, 0:20], T.cqo[:, ci:ci + 1], Op.add)
        do("v", "ofq phr row0", "row", lambda: V.tensor_copy(T.row[:].indirect(T.ofq[:, 0:20]), T.phr[:]))
        blend(1)
        if final:
            for a in range(2):
                do("v", "row", "tr", lambda: V.transpose(T.trl[:, a, :], T.row[:, 16 * a:16 * a + 320]), more=a > 0)
            blend(2)
            for a in range(2):
                ts("te%d" % a, "tr me", T.te[:, a:20:2], T.trl[:, a, 0:320:32], T.me[:, 0:1], Op.mult)
                ts("to%d" % a, "tr mo", T.to[:, a:20:2], T.trl[:, a, 16:320:32], T.mo[:, 0:1], Op.mult)
        else:
            for i in range(5):
                for a in range(2):
                    c = i + 80 * a
                    do("v", "row", "tr", lambda: V.transpose(T.tr[:, i, a, :], T.row[:, c:c + 316:5]), more=i + a > 0)
            blend(2)
            for h in range(2):
                sl = slice(10 * h, 10 * h + 10)
                ts("te%d" % h, "tr me", T.te[:, sl], T.tr[:, :, :, 32 * h], T.me[:, 0:1], Op.mult)
                ts("to%d" % h, "tr mo", T.to[:, sl], T.tr[:, :, :, 32 * h + 16], T.mo[:, 0:1], Op.mult)
        blend(3)
        tt("ql", "te0 te1 to0 to1", T.to[:], T.te[:], T.to[:], Op.add)
        copy("off0", "ql", T.off[:], T.to[:])

        def picks(h):
            o, cs = T.off[:, 10 * h:10 * h + 10], slice(640 * h, 640 * h + 640)
            for b in range(2):
                do("v", "off0 zp%d" % b, "zt%d" % h, lambda: V.tensor_copy(T.zt[:, 640 * h + b:640 * h + 640:4], T.zp[:, 320 * b:320 * b + 320].indirect(o)), more=b > 0)
            for b in range(2, 4):
                act("zt%d" % h, "off0 zp%d" % b, T.zt[:, 640 * h + b:640 * h + 640:4], T.zp[:, 320 * b:320 * b + 320].indirect(o), more=True)
            return cs

        def kept(h, b, e):
            o = T.off[:, 10 * h:10 * h + 10]
            out, win = T.at[:, 640 * h + b:640 * h + 640:4], T.tp[:, 320 * b:320 * b + 320].indirect(o)
            if e == "v":
                ts("at%d%d" % (h, b), "off0 tp", out, win, 2048.0, Op.mult)
            else:
                act("at%d%d" % (h, b), "off0 tp", out, win, 2048.0)

        def new(h, b, k, cod):
            mm("ps%d" % k, "wq " + cod[0], (ps[k][:, 0:160], T.wq[:, 128 * b:128 * b + 128], T.wsc[:, 128 * b:128 * b + 128], cod[1], cod[2]))

        def finish(h, b, k):
            tt("tm%d%d" % (h, b), "ps%d at%d%d" % (k, h, b), T.tm[:, 4 * h + b, :], ps[k][:, 0:160], T.at[:, 640 * h + b:640 * h + 640:4], Op.add)
            if final:
                act("xl%d" % h, "tm%d%d" % (h, b), T.xl[:, 640 * h + b:640 * h + 640:4], T.tm[:, 4 * h + b, :], 2.0 ** -11, more=b > 0)
            else:
                act("xt", "tm%d%d" % (h, b), T.xt[:, :, 32 * h:32 * h + 32, b], T.tm[:, 4 * h + b, :], 2.0 ** -11, more=h == 0 or b > 0)

        rc = slice(160 * t, 160 * t + 160)
        cs = picks(0)
        quant("sq%d" % t, "zt0", T.sendc[:, rc], T.sendp[:, rc], T.zt[:, cs])
        dst = partner_of(t)
        rid, pid, _ = topo.addr(dst)
        pre("p", "sq%d" % t, "")
        for a, b in ((T.landc[:, rc].bitcast(dt.uint8), T.sendc[:, rc].bitcast(dt.uint8)), (T.landp[:, rc], T.sendp[:, rc])):
            g.remote_dma(a, b, T.sem["arr%d" % t], T.sem["snd%d" % t], pid, rid, topo.mask(core, dst))
        eng = 2 * len(topo.engines(core, dst))
        last["land%d" % t] = {"arr%d" % t: eng}
        cs = picks(1)
        quant("stay%d" % t, "zt1", T.stayc[:, rc], T.stayp[:, rc], T.zt[:, cs])
        for b in range(4):
            new(1, b, 4 + b, ("stay%d" % t, T.stayc[:, rc], T.stayp[:, rc]))
        for h in (1, 0):
            for b in range(4):
                kept(h, b, "v" if b < 2 else "s")
            if h:
                for b in range(4):
                    finish(1, b, 4 + b)
        if t == 0:
            quant("vq", "vt", T.vq[:], T.vs[:], T.vt[:])
        if final:
            quant("lq1", "xl1", T.lq[:, 160:320], T.lsc[:, 160:320], T.xl[:, 640:1280])
            do("v", "ofq lgr row0", "row", lambda: V.tensor_copy(T.row[:].indirect(T.ofq[:, 0:20]), T.lgr[:]))
            mm("ps4", "lq1 vq", (ps[4][:, 0:160], T.vq[:], T.vs[:], T.lq[:, 160:320], T.lsc[:, 160:320]))
            do("y", "row", "", lambda: Y.dma_start(T.oq[0:8:2, :], T.row[0:128:32, 0:320]), "fin", 16)
            do("y", "row", "", lambda: Y.dma_start(T.oq[1:8:2, :], T.row[16:128:32, 16:336]), "fin", 16)
            do("y", "lq1", "", lambda: Y.dma_start(T.oc[:, 640:1280], T.lq[:, 160:320].bitcast(dt.uint8)), "fin", 16)
            copy("yb1", "ps4", T.yb[:, 160:320], ps[4][:, 0:160])
            do("y", "yb1", "", lambda: Y.dma_start(T.y[:, 160:320], T.yb[:, 160:320]), "fin", 16)
        for b in range(4):
            new(0, b, b, ("land%d" % t, T.landc[:, rc], T.landp[:, rc]))
        for b in range(4):
            finish(0, b, b)
        need("p", "snd%d" % t, eng)
        if not final:
            quant("xq", "xt xqz", T.xq[:, 0:320], T.xs[:, 0:320], T.xt[:])

    quant("lq0", "xl0", T.lq[:, 0:160], T.lsc[:, 0:160], T.xl[:, 0:640])
    mm("ps5", "lq0 vq", (ps[5][:, 0:160], T.vq[:], T.vs[:], T.lq[:, 0:160], T.lsc[:, 0:160]))
    do("y", "lq0", "", lambda: Y.dma_start(T.oc[:, 0:640], T.lq[:, 0:160].bitcast(dt.uint8)), "fin", 16)
    for k in range(4):
        q = ("s", S) if k % 2 else ("y", Y)
        do(q[0], "lq0 lq1", "", lambda: q[1].dma_start(T.osc[4 * k:4 * k + 4, :], T.lsc[32 * k:32 * k + 4, :]), "fin", 16)
    copy("yb0", "ps5", T.yb[:, 0:160], ps[5][:, 0:160])
    do("y", "yb0", "", lambda: Y.dma_start(T.y[:, 0:160], T.yb[:, 0:160]), "fin", 16)
    need("y", "fin", count["fin"])
    for k in ("v", "s", "t", "p"):
        need("y", k, count[k])
    for k in ("dx", "du", "dw", "dv"):
        need("y", k, count[k])
